import numpy as np
import ml_dtypes


def mxq(x, axis, fmt="e4m3"):
    dtype, down = {"e4m3": (ml_dtypes.float8_e4m3fn, 7), "e5m2": (ml_dtypes.float8_e5m2, 14)}[fmt]
    v = np.moveaxis(np.asarray(x, np.float32).astype(ml_dtypes.bfloat16).astype(np.float64), axis, -1)
    blocks = v.reshape(v.shape[:-1] + (-1, 32))
    amax = np.abs(blocks).max(-1, keepdims=True)
    byte = np.maximum(np.where(amax > 0, np.frexp(amax)[1] - 1 + 127, 0) - down, 1)
    scale = np.exp2(byte - 127.0)
    codes = (blocks / scale).astype(np.float32).astype(dtype).astype(np.float64)
    return np.moveaxis((codes * scale).reshape(v.shape), -1, axis)


WIDE = False


def mx_kscale(k):
    if not WIDE:
        return np.ones(k)
    levels = np.array([18, -18])
    if k % 512:
        return np.exp2(np.random.permutation(np.resize(levels, k // 32))).repeat(32)
    a = np.empty((k // 512, 16))
    for p in range(k // 512):
        a[p, :8] = np.random.permutation(np.resize(levels, 8))
        for g in range(8):
            far = levels[np.abs(levels - a[p, g]) >= 10]
            a[p, g + 8] = far[np.random.randint(len(far))]
    return np.exp2(a.ravel()).repeat(32)


def f64(x):
    return np.asarray(x).astype(np.float64)


def striped(idx):
    return np.tile(np.asarray(idx).reshape(-1, 16).T, (8, 1)).astype(np.uint16)


def unstriped(offs):
    return offs[:16].T.reshape(-1).astype(np.int64)


def setup_inputs():
    n = np.random.standard_normal
    uni = np.random.uniform
    idx = np.random.permutation(2048)[:512]
    f_d = mx_kscale(512)
    f_i = np.ones(2048)
    f_i[idx] = mx_kscale(512)
    return {
        "kT": (n((512, 2048)) * f_d[:, None] * f_i[None, :]).astype(np.float32),
        "vT": (n((512, 2048))).astype(np.float32),
        "W": (n((512, 512)) / np.sqrt(512) / f_d[:, None]).astype(np.float32),
        "ts": np.tile(uni(0.75, 1.3, 2048), (128, 1)).astype(np.float32),
        "tk": np.tile(uni(0.75, 1.3, 2048) / f_i, (128, 1)).astype(np.float32),
        "cf": (uni(0.75, 1.3, (512, 1))).astype(np.float32),
        "offs": striped(idx),
    }


def reference(kT, vT, W, ts, tk, cf, offs):
    idx = unstriped(offs)
    kT_i = f64(kT)[:, idx]
    v = f64(vT)[:, idx]
    ts_i = f64(ts)[:1][:, idx]
    tk_i = f64(tk)[:1][:, idx]
    u = mxq(f64(W), 0, "e4m3").T @ mxq(kT_i, 0, "e4m3")
    e = f64(cf) * ts_i * tk_i * (f64(cf) * tk_i * u - v)
    out = mxq(kT_i, 1, "e4m3") @ mxq(e, 1, "e5m2").T
    return out

@@ -1,0 +1,173 @@
+from contextlib import ExitStack
+
+import concourse.mybir as mybir
+from concourse.masks import make_identity
+
+P = 128
+PACK = 4
+N = 512
+T = 2048
+TILES = N // P
+VECTOR_COLS = 320
+LAST = P - 1
+
+FLOPS = 2 * 2 * N * N * N
+BYTES = 4 * (2 * N * T + 2 * N * N + 2 * T + N) + 2 * P * (N // 16)
+
+F32 = mybir.dt.float32
+BF16 = mybir.dt.bfloat16
+U32 = mybir.dt.uint32
+U16 = mybir.dt.uint16
+U8 = mybir.dt.uint8
+E4M3 = mybir.dt.float8_e4m3fn_x4
+E5M2 = mybir.dt.float8_e5m2_x4
+MULT = mybir.AluOpType.mult
+SUB = mybir.AluOpType.subtract
+COPY = mybir.ActivationFunctionType.Copy
+
+
+def interleave(nc, grouped, planes):
+    dst = grouped.rearrange("p (c i t) -> p c t i", i=4, t=PACK)
+    src = planes.rearrange("p (t c i) -> p c t i", t=PACK, i=4)
+    cut = VECTOR_COLS // 4
+    nc.vector.tensor_copy(dst[:, :cut], src[:, :cut])
+    nc.scalar.copy(dst[:, cut:], src[:, cut:])
+
+
+def tile_attend_gttt_W_kernel(tc, kT, vT, W, ts, tk, cf, offs, out):
+    nc = tc.nc
+    with ExitStack() as ctx:
+        sb = ctx.enter_context(tc.tile_pool(name="sb", bufs=1))
+        ps = ctx.enter_context(tc.psum_pool(name="ps", bufs=1))
+
+        def bank(group, j, name):
+            return ps.tile([P, N], F32, name=name, tag="bank_%s%d" % (group, j))
+
+        offsets = sb.tile([P, N // 16], U16, name="offsets")
+        nc.sync.dma_start(offsets[:], offs)
+
+        k_rows = kT.rearrange("(p t) n -> t p n", t=PACK)
+        k_win = [sb.tile([P, T], F32, name="k_win%d" % t) for t in range(PACK)]
+        v_win = [sb.tile([P, T], F32, name="v_win%d" % j) for j in range(TILES)]
+        w_raw = sb.tile([P, PACK * N], F32, name="w_raw")
+        tk_win = sb.tile([P, T], F32, name="tk_win")
+        ts_win = sb.tile([P, T], F32, name="ts_win")
+        cf_rows = sb.tile([P, P], F32, name="cf_rows")
+        ident = sb.tile([P, P], F32, name="ident")
+
+        nc.gpsimd.memset(cf_rows[: P - TILES, :], 0.0)
+        nc.vector.memset(tk_win[:LAST, :], 0.0)
+        nc.vector.memset(ts_win[:LAST, :], 0.0)
+        make_identity(nc, ident[:])
+        nc.scalar.dma_start(tk_win[LAST:, :], tk[0:1, :])
+        nc.scalar.dma_start(ts_win[LAST:, :], ts[0:1, :])
+        nc.scalar.dma_start(cf_rows[P - TILES :, :], cf.rearrange("(j p) o -> j (p o)", p=P))
+        for t in range(PACK):
+            nc.sync.dma_start(k_win[t][:], k_rows[t])
+        nc.sync.dma_start(w_raw[:], W.rearrange("(p t) f -> p (t f)", t=PACK))
+        for j in range(TILES):
+            nc.sync.dma_start(v_win[j][:], vT[j * P : (j + 1) * P, :])
+
+        def turn_pairs(src, group, j, name):
+            words = src.bitcast(F32)
+            turned = bank(group, j, name + "_ps")
+            for u in range(2):
+                nc.tensor.transpose(turned[:, u * P : (u + 1) * P], words[:, u : 2 * P : 2], ident[:])
+            dst = sb.tile([P, N], BF16, name=name, align_bytes=64)
+            nc.scalar.copy(
+                dst[:].bitcast(F32).rearrange("s (m u) -> s m u", u=2),
+                turned[:, : 2 * P].rearrange("s (u m) -> s m u", u=2),
+            )
+            return dst
+
+        cf_ps = bank("a", 2, "cf_ps")
+        nc.tensor.transpose(cf_ps[:, :P], cf_rows[:], ident[:])
+        cf_col = sb.tile([P, TILES], F32, name="cf_col")
+        nc.scalar.copy(cf_col[:], cf_ps[:, P - TILES : P])
+        cf_sq = sb.tile([P, TILES], F32, name="cf_sq")
+        nc.vector.tensor_tensor(cf_sq[:], cf_col[:], cf_col[:], MULT)
+
+        tk_row = sb.tile([P, N], F32, name="tk_row")
+        nc.vector.tensor_copy(tk_row[:], tk_win[:].indirect(offsets[:]))
+        a_row = sb.tile([P, N], F32, name="a_row")
+        nc.vector.tensor_tensor(a_row[:], ts_win[:].indirect(offsets[:]), tk_row[:], MULT)
+        a_ps = bank("a", 0, "a_ps")
+        tk_ps = bank("a", 1, "tk_ps")
+        for r in range(TILES):
+            nc.tensor.transpose(a_ps[:, r * P : (r + 1) * P], a_row[:, r * P : (r + 1) * P], ident[:])
+        for r in range(TILES):
+            nc.tensor.transpose(tk_ps[:, r * P : (r + 1) * P], tk_row[:, r * P : (r + 1) * P], ident[:])
+        a_col = sb.tile([P, TILES], F32, name="a_col")
+        nc.scalar.copy(a_col[:], a_ps[:, LAST:N:P])
+        b_col = sb.tile([P, TILES], F32, name="b_col")
+        for r in range(TILES):
+            nc.scalar.activation(b_col[:, r : r + 1], tk_ps[:, r * P + LAST : (r + 1) * P], COPY, scale=a_col[:, r : r + 1])
+        a_all = bank("a", 3, "a_all")
+        for r in range(TILES):
+            nc.tensor.transpose(a_all[:, r * P : (r + 1) * P], a_col[:, r : r + 1].to_broadcast([P, P]), ident[:])
+        cf_a = []
+        for j in range(TILES):
+            tile = sb.tile([P, N], F32, name="cf_a%d" % j)
+            nc.scalar.activation(tile[:], a_all[:], COPY, scale=cf_col[:, j : j + 1])
+            cf_a.append(tile)
+
+        k_planes = sb.tile([P, PACK * N], BF16, name="k_planes", align_bytes=64)
+        ki_codes = [sb.tile([P, P], U32, name="ki_codes%d" % t, align_bytes=64) for t in range(PACK)]
+        ki_scales = [sb.tile([P, P], U8, name="ki_scales%d" % t, align_bytes=64) for t in range(PACK)]
+        for t in range(PACK):
+            plane = k_planes[:, t * N : (t + 1) * N]
+            nc.vector.tensor_copy(plane, k_win[t][:].indirect(offsets[:]))
+            turned = turn_pairs(plane, "b", t, "k_turned%d" % t)
+            nc.vector.quantize_mx(ki_codes[t][:].bitcast(E4M3), ki_scales[t][:], turned[:])
+        kd_in = sb.tile([P, PACK * N], BF16, name="kd_in", align_bytes=64)
+        interleave(nc, kd_in[:], k_planes[:])
+        kd_codes = sb.tile([P, N], U32, name="kd_codes", align_bytes=64)
+        kd_scales = sb.tile([P, N], U8, name="kd_scales", align_bytes=64)
+        nc.vector.quantize_mx(kd_codes[:].bitcast(E4M3), kd_scales[:], kd_in[:])
+
+        w_in = sb.tile([P, PACK * N], BF16, name="w_in", align_bytes=64)
+        interleave(nc, w_in[:], w_raw[:])
+        w_codes = sb.tile([P, N], U32, name="w_codes", align_bytes=64)
+        w_scales = sb.tile([P, N], U8, name="w_scales", align_bytes=64)
+        nc.vector.quantize_mx(w_codes[:].bitcast(E4M3), w_scales[:], w_in[:])
+
+        ub = []
+        for r in range(TILES):
+            u_ps = bank("a", r, "u_ps%d" % r)
+            cols = slice(r * P, (r + 1) * P)
+            nc.tensor.matmul_mx(
+                out=u_ps[:], lhsT=kd_codes[:, cols].bitcast(E4M3), lhsT_scale=kd_scales[:, cols],
+                rhs=w_codes[:].bitcast(E4M3), rhs_scale=w_scales[:], start=True, stop=True,
+            )
+            tile = sb.tile([P, N], F32, name="ub%d" % r)
+            nc.scalar.activation(tile[:], u_ps[:], COPY, scale=b_col[:, r : r + 1])
+            ub.append(tile)
+        ub_turned = [bank("b", j, "ub_turned%d" % j) for j in range(TILES)]
+        for r in range(TILES):
+            for j in range(TILES):
+                nc.tensor.transpose(ub_turned[j][:, r * P : (r + 1) * P], ub[r][:, j * P : (j + 1) * P], ident[:])
+
+        e_codes = sb.tile([P, N], U32, name="e_codes", align_bytes=64)
+        e_scales = sb.tile([P, N], U8, name="e_scales", align_bytes=64)
+        for j in range(TILES):
+            va = sb.tile([P, N], F32, name="va%d" % j)
+            nc.vector.tensor_tensor(va[:], v_win[j][:].indirect(offsets[:]), cf_a[j][:], MULT)
+            e = sb.tile([P, N], BF16, name="e%d" % j, align_bytes=64)
+            nc.vector.scalar_tensor_tensor(e[:], ub_turned[j][:], cf_sq[:, j : j + 1], va[:], MULT, SUB)
+            turned = turn_pairs(e[:], "b", j, "e_turned%d" % j)
+            cols = slice(j * P, (j + 1) * P)
+            nc.vector.quantize_mx(e_codes[:, cols].bitcast(E5M2), e_scales[:, cols], turned[:])
+
+        out_rows = out.rearrange("(p t) f -> t p f", t=PACK)
+        for t in range(PACK):
+            o_ps = bank("a", t, "o_ps%d" % t)
+            nc.tensor.matmul_mx(
+                out=o_ps[:], lhsT=ki_codes[t][:].bitcast(E4M3), lhsT_scale=ki_scales[t][:],
+                rhs=e_codes[:].bitcast(E5M2), rhs_scale=e_scales[:], start=True, stop=True,
+            )
+            o_sb = sb.tile([P, N], F32, name="o_sb%d" % t)
+            if t % 2 == 0:
+                nc.scalar.copy(o_sb[:], o_ps[:])
+            else:
+                nc.vector.tensor_copy(o_sb[:], o_ps[:])
+            nc.sync.dma_start(out_rows[t], o_sb[:])

@@ -8,7 +8,7 @@ PACK = 4
 N = 512
 T = 2048
 TILES = N // P
-VECTOR_COLS = 320
+VECTOR_COLS = 192
 LAST = P - 1
 
 FLOPS = 2 * 2 * N * N * N
@@ -22,7 +22,7 @@ U8 = mybir.dt.uint8
 E4M3 = mybir.dt.float8_e4m3fn_x4
 E5M2 = mybir.dt.float8_e5m2_x4
 MULT = mybir.AluOpType.mult
-SUB = mybir.AluOpType.subtract
+ADD = mybir.AluOpType.add
 COPY = mybir.ActivationFunctionType.Copy
 
 
@@ -34,6 +34,13 @@ def interleave(nc, grouped, planes):
     nc.scalar.copy(dst[:, cut:], src[:, cut:])
 
 
+def interleave_dealt(nc, grouped, planes):
+    dst = grouped.rearrange("p (r s t) -> p s r t", r=PACK, t=PACK)
+    src = planes.rearrange("p (t s r) -> p s r t", t=PACK, r=PACK)
+    nc.vector.tensor_copy(dst[:, :, : PACK - 1], src[:, :, : PACK - 1])
+    nc.scalar.copy(dst[:, :, PACK - 1 :], src[:, :, PACK - 1 :])
+
+
 def tile_attend_gttt_W_kernel(tc, kT, vT, W, ts, tk, cf, offs, out):
     nc = tc.nc
     with ExitStack() as ctx:
@@ -43,15 +50,18 @@ def tile_attend_gttt_W_kernel(tc, kT, vT, W, ts, tk, cf, offs, out):
         def bank(group, j, name):
             return ps.tile([P, N], F32, name=name, tag="bank_%s%d" % (group, j))
 
+        def tile(cols, dtype, name, tag=None):
+            return sb.tile([P, cols], dtype, name=name, tag=tag or name, align_bytes=64)
+
         offsets = sb.tile([P, N // 16], U16, name="offsets")
         nc.sync.dma_start(offsets[:], offs)
 
         k_rows = kT.rearrange("(p t) n -> t p n", t=PACK)
-        k_win = [sb.tile([P, T], F32, name="k_win%d" % t) for t in range(PACK)]
+        k_win = [tile(T, F32, "k_win%d" % t) for t in range(PACK)]
         v_win = [sb.tile([P, T], F32, name="v_win%d" % j) for j in range(TILES)]
-        w_raw = sb.tile([P, PACK * N], F32, name="w_raw")
+        w_raw = tile(PACK * N, F32, "w_raw")
         tk_win = sb.tile([P, T], F32, name="tk_win")
-        ts_win = sb.tile([P, T], F32, name="ts_win")
+        ts_win = tile(T, F32, "ts_win")
         cf_rows = sb.tile([P, P], F32, name="cf_rows")
         ident = sb.tile([P, P], F32, name="ident")
 
@@ -73,17 +83,18 @@ def tile_attend_gttt_W_kernel(tc, kT, vT, W, ts, tk, cf, offs, out):
             turned = bank(group, j, name + "_ps")
             for u in range(2):
                 nc.tensor.transpose(turned[:, u * P : (u + 1) * P], words[:, u : 2 * P : 2], ident[:])
-            dst = sb.tile([P, N], BF16, name=name, align_bytes=64)
+            return turned
+
+        def weave_pairs(dst, turned):
             nc.scalar.copy(
-                dst[:].bitcast(F32).rearrange("s (m u) -> s m u", u=2),
+                dst.bitcast(F32).rearrange("s (m u) -> s m u", u=2),
                 turned[:, : 2 * P].rearrange("s (u m) -> s m u", u=2),
             )
-            return dst
 
         cf_ps = bank("a", 2, "cf_ps")
         nc.tensor.transpose(cf_ps[:, :P], cf_rows[:], ident[:])
         cf_col = sb.tile([P, TILES], F32, name="cf_col")
-        nc.scalar.copy(cf_col[:], cf_ps[:, P - TILES : P])
+        nc.scalar.activation(cf_col[:], cf_ps[:, P - TILES : P], COPY, scale=-1.0)
         cf_sq = sb.tile([P, TILES], F32, name="cf_sq")
         nc.vector.tensor_tensor(cf_sq[:], cf_col[:], cf_col[:], MULT)
 
@@ -94,9 +105,9 @@ def tile_attend_gttt_W_kernel(tc, kT, vT, W, ts, tk, cf, offs, out):
         a_ps = bank("a", 0, "a_ps")
         tk_ps = bank("a", 1, "tk_ps")
         for r in range(TILES):
-            nc.tensor.transpose(a_ps[:, r * P : (r + 1) * P], a_row[:, r * P : (r + 1) * P], ident[:])
+            nc.tensor.transpose(a_ps[:, r * P : (r + 1) * P], a_row[:, r:N:PACK], ident[:])
         for r in range(TILES):
-            nc.tensor.transpose(tk_ps[:, r * P : (r + 1) * P], tk_row[:, r * P : (r + 1) * P], ident[:])
+            nc.tensor.transpose(tk_ps[:, r * P : (r + 1) * P], tk_row[:, r:N:PACK], ident[:])
         a_col = sb.tile([P, TILES], F32, name="a_col")
         nc.scalar.copy(a_col[:], a_ps[:, LAST:N:P])
         b_col = sb.tile([P, TILES], F32, name="b_col")
@@ -106,30 +117,49 @@ def tile_attend_gttt_W_kernel(tc, kT, vT, W, ts, tk, cf, offs, out):
         for r in range(TILES):
             nc.tensor.transpose(a_all[:, r * P : (r + 1) * P], a_col[:, r : r + 1].to_broadcast([P, P]), ident[:])
         cf_a = []
-        for j in range(TILES):
-            tile = sb.tile([P, N], F32, name="cf_a%d" % j)
-            nc.scalar.activation(tile[:], a_all[:], COPY, scale=cf_col[:, j : j + 1])
-            cf_a.append(tile)
 
-        k_planes = sb.tile([P, PACK * N], BF16, name="k_planes", align_bytes=64)
-        ki_codes = [sb.tile([P, P], U32, name="ki_codes%d" % t, align_bytes=64) for t in range(PACK)]
-        ki_scales = [sb.tile([P, P], U8, name="ki_scales%d" % t, align_bytes=64) for t in range(PACK)]
+        def value_factor(j, dst):
+            cf_a.append(dst)
+            nc.scalar.activation(
+                dst.rearrange("p (s r) -> p s r", r=PACK),
+                a_all[:].rearrange("p (r s) -> p s r", r=PACK),
+                COPY,
+                scale=cf_col[:, j : j + 1],
+            )
+
+        for j in range(2):
+            value_factor(j, tile(N, F32, "cf_a%d" % j)[:])
+
+        k_planes = tile(PACK * N, BF16, "k_planes", tag="ts_win")
+        k_turned = [tile(2 * N, BF16, "k_turned0")[:]]
+        late_turns = []
         for t in range(PACK):
             plane = k_planes[:, t * N : (t + 1) * N]
             nc.vector.tensor_copy(plane, k_win[t][:].indirect(offsets[:]))
-            turned = turn_pairs(plane, "b", t, "k_turned%d" % t)
-            nc.vector.quantize_mx(ki_codes[t][:].bitcast(E4M3), ki_scales[t][:], turned[:])
-        kd_in = sb.tile([P, PACK * N], BF16, name="kd_in", align_bytes=64)
-        interleave(nc, kd_in[:], k_planes[:])
-        kd_codes = sb.tile([P, N], U32, name="kd_codes", align_bytes=64)
-        kd_scales = sb.tile([P, N], U8, name="kd_scales", align_bytes=64)
-        nc.vector.quantize_mx(kd_codes[:].bitcast(E4M3), kd_scales[:], kd_in[:])
-
-        w_in = sb.tile([P, PACK * N], BF16, name="w_in", align_bytes=64)
+            turned = turn_pairs(plane, "b", t, "k_turn%d" % t)
+            if t < 2:
+                weave_pairs(k_turned[0][:, t * N : (t + 1) * N], turned)
+            else:
+                late_turns.append(turned)
+        ki_scales = [tile(2 * P, U8, "ki_scales%d" % h) for h in range(2)]
+        kd_in = tile(PACK * N, BF16, "kd_in")
+        interleave_dealt(nc, kd_in[:], k_planes[:])
+        w_in = tile(PACK * N, BF16, "w_in")
         interleave(nc, w_in[:], w_raw[:])
+        late = tile(3 * N, F32, "late", tag="w_raw")
+        k_turned.append(late[:, 2 * N :].bitcast(BF16))
+        for h, turned in enumerate(late_turns):
+            weave_pairs(k_turned[1][:, h * N : (h + 1) * N], turned)
+        kd_codes = tile(N, U32, "kd_codes")
+        kd_scales = tile(N, U8, "kd_scales")
+        nc.vector.quantize_mx(kd_codes[:].bitcast(E4M3), kd_scales[:], kd_in[:])
+        for j in range(2, TILES):
+            value_factor(j, late[:, (j - 2) * N : (j - 1) * N])
+
         w_codes = sb.tile([P, N], U32, name="w_codes", align_bytes=64)
         w_scales = sb.tile([P, N], U8, name="w_scales", align_bytes=64)
         nc.vector.quantize_mx(w_codes[:].bitcast(E4M3), w_scales[:], w_in[:])
+
 
         ub = []
         for r in range(TILES):
@@ -139,35 +169,83 @@ def tile_attend_gttt_W_kernel(tc, kT, vT, W, ts, tk, cf, offs, out):
                 out=u_ps[:], lhsT=kd_codes[:, cols].bitcast(E4M3), lhsT_scale=kd_scales[:, cols],
                 rhs=w_codes[:].bitcast(E4M3), rhs_scale=w_scales[:], start=True, stop=True,
             )
-            tile = sb.tile([P, N], F32, name="ub%d" % r)
-            nc.scalar.activation(tile[:], u_ps[:], COPY, scale=b_col[:, r : r + 1])
-            ub.append(tile)
+            ub.append(tile(N, F32, "ub%d" % r))
+            nc.scalar.activation(ub[r][:], u_ps[:], COPY, scale=b_col[:, r : r + 1])
         ub_turned = [bank("b", j, "ub_turned%d" % j) for j in range(TILES)]
         for r in range(TILES):
             for j in range(TILES):
                 nc.tensor.transpose(ub_turned[j][:, r * P : (r + 1) * P], ub[r][:, j * P : (j + 1) * P], ident[:])
 
-        e_codes = sb.tile([P, N], U32, name="e_codes", align_bytes=64)
-        e_scales = sb.tile([P, N], U8, name="e_scales", align_bytes=64)
-        for j in range(TILES):
-            va = sb.tile([P, N], F32, name="va%d" % j)
-            nc.vector.tensor_tensor(va[:], v_win[j][:].indirect(offsets[:]), cf_a[j][:], MULT)
-            e = sb.tile([P, N], BF16, name="e%d" % j, align_bytes=64)
-            nc.vector.scalar_tensor_tensor(e[:], ub_turned[j][:], cf_sq[:, j : j + 1], va[:], MULT, SUB)
-            turned = turn_pairs(e[:], "b", j, "e_turned%d" % j)
-            cols = slice(j * P, (j + 1) * P)
-            nc.vector.quantize_mx(e_codes[:, cols].bitcast(E5M2), e_scales[:, cols], turned[:])
+        va = [tile(N, F32, "va%d" % j) for j in range(TILES)]
+        e_turned = [tile(2 * N, BF16, "e_turned01"), tile(N, BF16, "e_turned2"), tile(N, BF16, "e_turned3")]
+        e_dst = [e_turned[0][:, :N], e_turned[0][:, N:], e_turned[1][:], e_turned[2][:]]
+
+        def gather_values(j):
+            nc.vector.tensor_tensor(va[j][:], v_win[j][:].indirect(offsets[:]), cf_a[j], MULT)
+
+        ki_codes = []
+
+        def quantize_turned_keys(h):
+            ki_codes.append(tile(2 * P, U32, "ki_codes%d" % h, tag="cf_a%d" % h))
+            nc.vector.quantize_mx(ki_codes[h][:].bitcast(E4M3), ki_scales[h][:], k_turned[h])
+
+        def residual_on_vector(j):
+            turned = bank("a", j, "e_turn%d" % j)
+            for u in range(2):
+                e = tile(2 * P, BF16, "e%d_%d" % (j, u))
+                nc.vector.scalar_tensor_tensor(
+                    e[:].rearrange("p (s r) -> p s r", r=2),
+                    ub_turned[j][:].rearrange("p (r s) -> p s r", r=PACK)[:, :, 2 * u : 2 * u + 2],
+                    cf_sq[:, j : j + 1],
+                    va[j][:].rearrange("p (s r) -> p s r", r=PACK)[:, :, 2 * u : 2 * u + 2],
+                    MULT,
+                    ADD,
+                )
+                nc.tensor.transpose(turned[:, u * P : (u + 1) * P], e[:].bitcast(F32), ident[:])
+            weave_pairs(e_dst[j], turned)
+
+        def residual_on_tensor(j):
+            fitted = tile(N, F32, "fitted%d" % j)
+            nc.scalar.activation(fitted[:], ub_turned[j][:], COPY, scale=cf_sq[:, j : j + 1])
+            total = bank("a", j, "e_sum%d" % j)
+            for r in range(PACK):
+                cols = slice(r * P, (r + 1) * P)
+                nc.tensor.matmul(total[:, cols], fitted[:, cols], ident[:], start=True, stop=False, is_transpose=True)
+                nc.tensor.matmul(total[:, cols], va[j][:, r:N:PACK], ident[:], start=False, stop=True, is_transpose=True)
+            nc.scalar.copy(
+                e_dst[j].rearrange("s (m r) -> s m r", r=PACK), total[:].rearrange("s (r m) -> s m r", r=PACK)
+            )
+
+        gather_values(0)
+        quantize_turned_keys(0)
+        residual_on_tensor(0)
+        gather_values(1)
+        quantize_turned_keys(1)
+        residual_on_tensor(1)
+        for j in range(2, TILES):
+            gather_values(j)
+            residual_on_vector(j)
+
+        e_codes = tile(N, U32, "e_codes", tag="va3")
+        e_scales = tile(N, U8, "e_scales")
+        start = 0
+        for part in e_turned:
+            cols = slice(start, start + part.shape[1] // PACK)
+            nc.vector.quantize_mx(e_codes[:, cols].bitcast(E5M2), e_scales[:, cols], part[:])
+            start = cols.stop
 
         out_rows = out.rearrange("(p t) f -> t p f", t=PACK)
         for t in range(PACK):
-            o_ps = bank("a", t, "o_ps%d" % t)
+            o_ps = bank("b", t, "o_ps%d" % t)
+            cols = slice((t % 2) * P, (t % 2 + 1) * P)
             nc.tensor.matmul_mx(
-                out=o_ps[:], lhsT=ki_codes[t][:].bitcast(E4M3), lhsT_scale=ki_scales[t][:],
+                out=o_ps[:], lhsT=ki_codes[t // 2][:, cols].bitcast(E4M3), lhsT_scale=ki_scales[t // 2][:, cols],
                 rhs=e_codes[:].bitcast(E5M2), rhs_scale=e_scales[:], start=True, stop=True,
             )
-            o_sb = sb.tile([P, N], F32, name="o_sb%d" % t)
-            if t % 2 == 0:
-                nc.scalar.copy(o_sb[:], o_ps[:])
-            else:
-                nc.vector.tensor_copy(o_sb[:], o_ps[:])
-            nc.sync.dma_start(out_rows[t], o_sb[:])
+            for h, cols in enumerate([slice(0, N // 2), slice(N // 2, N)] if t == 0 else [slice(0, N)]):
+                o_sb = tile(cols.stop - cols.start, F32, "o_sb%d_%d" % (t, h))
+                if t % 2 == 0:
+                    nc.scalar.copy(o_sb[:], o_ps[:, cols])
+                else:
+                    nc.vector.tensor_copy(o_sb[:], o_ps[:, cols])
+                nc.sync.dma_start(out_rows[t][:, cols], o_sb[:])

@@ -8,8 +8,10 @@ PACK = 4
 N = 512
 T = 2048
 TILES = N // P
-VECTOR_COLS = 192
+HALF = N // 2
+VECTOR_SLOTS = 336
 LAST = P - 1
+EARLY_PLANES = (2, 3)
 
 FLOPS = 2 * 2 * N * N * N
 BYTES = 4 * (2 * N * T + 2 * N * N + 2 * T + N) + 2 * P * (N // 16)
@@ -26,26 +28,21 @@ ADD = mybir.AluOpType.add
 COPY = mybir.ActivationFunctionType.Copy
 
 
-def interleave(nc, grouped, planes):
+def interleaved(grouped, planes):
     dst = grouped.rearrange("p (c i t) -> p c t i", i=4, t=PACK)
-    src = planes.rearrange("p (t c i) -> p c t i", t=PACK, i=4)
-    cut = VECTOR_COLS // 4
-    nc.vector.tensor_copy(dst[:, :cut], src[:, :cut])
-    nc.scalar.copy(dst[:, cut:], src[:, cut:])
-
-
-def interleave_dealt(nc, grouped, planes):
-    dst = grouped.rearrange("p (r s t) -> p s r t", r=PACK, t=PACK)
-    src = planes.rearrange("p (t s r) -> p s r t", t=PACK, r=PACK)
-    nc.vector.tensor_copy(dst[:, :, : PACK - 1], src[:, :, : PACK - 1])
-    nc.scalar.copy(dst[:, :, PACK - 1 :], src[:, :, PACK - 1 :])
+    src = planes.rearrange("p t (c i) -> p c t i", i=4)
+    return dst, src
 
 
 def tile_attend_gttt_W_kernel(tc, kT, vT, W, ts, tk, cf, offs, out):
     nc = tc.nc
     with ExitStack() as ctx:
         sb = ctx.enter_context(tc.tile_pool(name="sb", bufs=1))
+        reuse = ctx.enter_context(tc.tile_pool(name="reuse", bufs=1))
         ps = ctx.enter_context(tc.psum_pool(name="ps", bufs=1))
+
+        def placed(cols, dtype, name, at):
+            return reuse.tile([P, cols], dtype, name=name, align_bytes=64, offset=512 * at)
 
         def bank(group, j, name):
             return ps.tile([P, N], F32, name=name, tag="bank_%s%d" % (group, j))
@@ -58,17 +55,17 @@ def tile_attend_gttt_W_kernel(tc, kT, vT, W, ts, tk, cf, offs, out):
 
         k_rows = kT.rearrange("(p t) n -> t p n", t=PACK)
         k_win = [tile(T, F32, "k_win%d" % t) for t in range(PACK)]
-        v_win = [sb.tile([P, T], F32, name="v_win%d" % j) for j in range(TILES)]
+        v_win = [tile(T, F32, "v_win%d" % j) for j in range(TILES)]
         w_raw = tile(PACK * N, F32, "w_raw")
-        tk_win = sb.tile([P, T], F32, name="tk_win")
+        tk_win = tile(T, F32, "tk_win")
         ts_win = tile(T, F32, "ts_win")
-        cf_rows = sb.tile([P, P], F32, name="cf_rows")
-        ident = sb.tile([P, P], F32, name="ident")
+        cf_rows = tile(P, F32, "cf_rows")
+        ident = tile(P, F32, "ident")
 
         nc.gpsimd.memset(cf_rows[: P - TILES, :], 0.0)
         nc.vector.memset(tk_win[:LAST, :], 0.0)
-        nc.vector.memset(ts_win[:LAST, :], 0.0)
         make_identity(nc, ident[:])
+        nc.gpsimd.memset(ts_win[:LAST, :], 0.0)
         nc.scalar.dma_start(tk_win[LAST:, :], tk[0:1, :])
         nc.scalar.dma_start(ts_win[LAST:, :], ts[0:1, :])
         nc.scalar.dma_start(cf_rows[P - TILES :, :], cf.rearrange("(j p) o -> j (p o)", p=P))
@@ -78,12 +75,14 @@ def tile_attend_gttt_W_kernel(tc, kT, vT, W, ts, tk, cf, offs, out):
         for j in range(TILES):
             nc.sync.dma_start(v_win[j][:], vT[j * P : (j + 1) * P, :])
 
-        def turn_pairs(src, group, j, name):
+        def turn_pairs(src, turned):
             words = src.bitcast(F32)
-            turned = bank(group, j, name + "_ps")
             for u in range(2):
                 nc.tensor.transpose(turned[:, u * P : (u + 1) * P], words[:, u : 2 * P : 2], ident[:])
-            return turned
+
+        def turn_row(row, turned):
+            for c in range(TILES):
+                nc.tensor.transpose(turned[:, c * P : (c + 1) * P], row[:, c * P : (c + 1) * P], ident[:])
 
         def weave_pairs(dst, turned):
             nc.scalar.copy(
@@ -91,161 +90,193 @@ def tile_attend_gttt_W_kernel(tc, kT, vT, W, ts, tk, cf, offs, out):
                 turned[:, : 2 * P].rearrange("s (u m) -> s m u", u=2),
             )
 
-        cf_ps = bank("a", 2, "cf_ps")
-        nc.tensor.transpose(cf_ps[:, :P], cf_rows[:], ident[:])
-        cf_col = sb.tile([P, TILES], F32, name="cf_col")
-        nc.scalar.activation(cf_col[:], cf_ps[:, P - TILES : P], COPY, scale=-1.0)
-        cf_sq = sb.tile([P, TILES], F32, name="cf_sq")
-        nc.vector.tensor_tensor(cf_sq[:], cf_col[:], cf_col[:], MULT)
+        k_planes = placed(PACK * N, BF16, "k_planes", 5)
+        k_turned = [k_planes[:, 2 * N : 3 * N], k_planes[:, 3 * N :], tile(N, BF16, "k_turned2")[:], placed(N, BF16, "k_turned3", 10)[:]]
+        ki_codes, ki_scales = [], []
 
-        tk_row = sb.tile([P, N], F32, name="tk_row")
-        nc.vector.tensor_copy(tk_row[:], tk_win[:].indirect(offsets[:]))
-        a_row = sb.tile([P, N], F32, name="a_row")
-        nc.vector.tensor_tensor(a_row[:], ts_win[:].indirect(offsets[:]), tk_row[:], MULT)
-        a_ps = bank("a", 0, "a_ps")
-        tk_ps = bank("a", 1, "tk_ps")
-        for r in range(TILES):
-            nc.tensor.transpose(a_ps[:, r * P : (r + 1) * P], a_row[:, r:N:PACK], ident[:])
-        for r in range(TILES):
-            nc.tensor.transpose(tk_ps[:, r * P : (r + 1) * P], tk_row[:, r:N:PACK], ident[:])
-        a_col = sb.tile([P, TILES], F32, name="a_col")
-        nc.scalar.copy(a_col[:], a_ps[:, LAST:N:P])
-        b_col = sb.tile([P, TILES], F32, name="b_col")
-        for r in range(TILES):
-            nc.scalar.activation(b_col[:, r : r + 1], tk_ps[:, r * P + LAST : (r + 1) * P], COPY, scale=a_col[:, r : r + 1])
-        a_all = bank("a", 3, "a_all")
-        for r in range(TILES):
-            nc.tensor.transpose(a_all[:, r * P : (r + 1) * P], a_col[:, r : r + 1].to_broadcast([P, P]), ident[:])
-        cf_a = []
+        def quantize_turned_keys(t, scales):
+            ki_codes.append(tile(P, U32, "ki_codes%d" % t))
+            ki_scales.append(scales)
+            nc.vector.quantize_mx(ki_codes[t][:].bitcast(E4M3), ki_scales[t][:], k_turned[t])
 
-        def value_factor(j, dst):
-            cf_a.append(dst)
-            nc.scalar.activation(
-                dst.rearrange("p (s r) -> p s r", r=PACK),
-                a_all[:].rearrange("p (r s) -> p s r", r=PACK),
-                COPY,
-                scale=cf_col[:, j : j + 1],
-            )
-
-        for j in range(2):
-            value_factor(j, tile(N, F32, "cf_a%d" % j)[:])
-
-        k_planes = tile(PACK * N, BF16, "k_planes", tag="ts_win")
-        k_turned = [tile(2 * N, BF16, "k_turned0")[:]]
-        late_turns = []
-        for t in range(PACK):
+        def gather_keys(t):
             plane = k_planes[:, t * N : (t + 1) * N]
             nc.vector.tensor_copy(plane, k_win[t][:].indirect(offsets[:]))
-            turned = turn_pairs(plane, "b", t, "k_turn%d" % t)
-            if t < 2:
-                weave_pairs(k_turned[0][:, t * N : (t + 1) * N], turned)
-            else:
-                late_turns.append(turned)
-        ki_scales = [tile(2 * P, U8, "ki_scales%d" % h) for h in range(2)]
+            if t > 0:
+                quantize_turned_keys(t - 1, tile(P, U8, "ki_scales%d" % (t - 1), tag="k_win%d" % t))
+            turned = bank("e", t, "k_turn%d" % t)
+            turn_pairs(plane, turned)
+            if t < PACK - 1:
+                weave_pairs(k_turned[t], turned)
+            return turned
+
+        tk_row = tile(N, F32, "tk_row")
+        nc.vector.tensor_copy(tk_row[:], tk_win[:].indirect(offsets[:]))
+        tk_ps = bank("a", 0, "tk_ps")
+        turn_row(tk_row, tk_ps)
+        gather_keys(0)
+        a_row = tile(N, F32, "a_row")
+        nc.vector.tensor_tensor(a_row[:], ts_win[:].indirect(offsets[:]), tk_row[:], MULT)
+        a_ps = bank("a", 1, "a_ps")
+        turn_row(a_row, a_ps)
+        a_col = tile(TILES, F32, "a_col")
+        nc.scalar.copy(a_col[:], a_ps[:, LAST:N:P])
+        b_col = tile(TILES, F32, "b_col")
+        for c in range(TILES):
+            nc.scalar.activation(b_col[:, c : c + 1], tk_ps[:, c * P + LAST : (c + 1) * P], COPY, scale=a_col[:, c : c + 1])
+
+        gather_keys(1)
+
+        cf_ps = bank("e", 3, "cf_ps")
+        nc.tensor.transpose(cf_ps[:, :P], cf_rows[:], ident[:])
+        cf_neg = tile(TILES, F32, "cf_neg")
+        nc.scalar.activation(cf_neg[:], cf_ps[:, P - TILES : P], COPY, scale=-1.0)
+        cf_sq = [tile(1, F32, "cf_sq%d" % j) for j in range(TILES)]
+        for j in range(TILES):
+            nc.scalar.activation(cf_sq[j][:], cf_neg[:, j : j + 1], COPY, scale=cf_neg[:, j : j + 1])
+
+        a_all_ps = bank("a", 2, "a_all_ps")
+        b_all_ps = bank("a", 3, "b_all_ps")
+        for col, spread in ((a_col, a_all_ps), (b_col, b_all_ps)):
+            for c in range(TILES):
+                nc.tensor.transpose(spread[:, c * P : (c + 1) * P], col[:, c : c + 1].to_broadcast([P, P]), ident[:])
+        a_all = tile(N, F32, "a_all")
+        nc.scalar.copy(a_all[:], a_all_ps[:])
+
+        gather_keys(2)
+
+        b_dealt = tile(N, F32, "b_dealt")
+        nc.scalar.copy(
+            b_dealt[:].rearrange("p (r s) -> p r s", r=PACK), b_all_ps[:].rearrange("p (s r) -> p r s", r=PACK)
+        )
+        b_all = tile(N, F32, "b_all")
+        nc.scalar.copy(b_all[:], b_all_ps[:])
+
+        last_turn = gather_keys(3)
+
         kd_in = tile(PACK * N, BF16, "kd_in")
-        interleave_dealt(nc, kd_in[:], k_planes[:])
-        w_in = tile(PACK * N, BF16, "w_in")
-        interleave(nc, w_in[:], w_raw[:])
-        late = tile(3 * N, F32, "late", tag="w_raw")
-        k_turned.append(late[:, 2 * N :].bitcast(BF16))
-        for h, turned in enumerate(late_turns):
-            weave_pairs(k_turned[1][:, h * N : (h + 1) * N], turned)
+        dst, src = interleaved(kd_in[:], k_planes[:].rearrange("p (t n) -> p t n", t=PACK))
+        cut = VECTOR_SLOTS // 4
+        nc.vector.tensor_copy(dst[:, :cut], src[:, :cut])
+        nc.scalar.copy(dst[:, cut:], src[:, cut:])
         kd_codes = tile(N, U32, "kd_codes")
         kd_scales = tile(N, U8, "kd_scales")
         nc.vector.quantize_mx(kd_codes[:].bitcast(E4M3), kd_scales[:], kd_in[:])
-        for j in range(2, TILES):
-            value_factor(j, late[:, (j - 2) * N : (j - 1) * N])
 
-        w_codes = sb.tile([P, N], U32, name="w_codes", align_bytes=64)
-        w_scales = sb.tile([P, N], U8, name="w_scales", align_bytes=64)
-        nc.vector.quantize_mx(w_codes[:].bitcast(E4M3), w_scales[:], w_in[:])
-
-
-        ub = []
-        for r in range(TILES):
-            u_ps = bank("a", r, "u_ps%d" % r)
-            cols = slice(r * P, (r + 1) * P)
+        w_planes = w_raw[:].rearrange("p (t f) -> p t f", t=PACK)
+        u_ps = []
+        for j in range(TILES):
+            w_in = placed(N, BF16, "w_in%d" % j, (8, 2, 0, 4)[j] + 4)[:]
+            dst, src = interleaved(w_in, w_planes[:, :, j * P : (j + 1) * P])
+            nc.scalar.copy(dst, src)
+            w_codes = tile(P, U32, "w_codes%d" % j)
+            w_scales = tile(P, U8, "w_scales%d" % j)
+            nc.vector.quantize_mx(w_codes[:].bitcast(E4M3), w_scales[:], w_in)
+            u_ps.append(bank("a", j, "u_ps%d" % j))
             nc.tensor.matmul_mx(
-                out=u_ps[:], lhsT=kd_codes[:, cols].bitcast(E4M3), lhsT_scale=kd_scales[:, cols],
-                rhs=w_codes[:].bitcast(E4M3), rhs_scale=w_scales[:], start=True, stop=True,
+                out=u_ps[j][:], lhsT=w_codes[:].bitcast(E4M3), lhsT_scale=w_scales[:],
+                rhs=kd_codes[:].bitcast(E4M3), rhs_scale=kd_scales[:], start=True, stop=True,
             )
-            ub.append(tile(N, F32, "ub%d" % r))
-            nc.scalar.activation(ub[r][:], u_ps[:], COPY, scale=b_col[:, r : r + 1])
-        ub_turned = [bank("b", j, "ub_turned%d" % j) for j in range(TILES)]
-        for r in range(TILES):
-            for j in range(TILES):
-                nc.tensor.transpose(ub_turned[j][:, r * P : (r + 1) * P], ub[r][:, j * P : (j + 1) * P], ident[:])
+        weave_pairs(k_turned[PACK - 1], last_turn)
 
-        va = [tile(N, F32, "va%d" % j) for j in range(TILES)]
-        e_turned = [tile(2 * N, BF16, "e_turned01"), tile(N, BF16, "e_turned2"), tile(N, BF16, "e_turned3")]
-        e_dst = [e_turned[0][:, :N], e_turned[0][:, N:], e_turned[1][:], e_turned[2][:]]
+        e_in = [tile(2 * N, BF16, "e_in01"), tile(N, BF16, "e_in2"), tile(N, BF16, "e_in3")]
+        e_dst = [e_in[0][:, :N], e_in[0][:, N:], e_in[1][:], e_in[2][:]]
+        sums = {}
 
-        def gather_values(j):
-            nc.vector.tensor_tensor(va[j][:], v_win[j][:].indirect(offsets[:]), cf_a[j], MULT)
-
-        ki_codes = []
-
-        def quantize_turned_keys(h):
-            ki_codes.append(tile(2 * P, U32, "ki_codes%d" % h, tag="cf_a%d" % h))
-            nc.vector.quantize_mx(ki_codes[h][:].bitcast(E4M3), ki_scales[h][:], k_turned[h])
-
-        def residual_on_vector(j):
-            turned = bank("a", j, "e_turn%d" % j)
-            for u in range(2):
-                e = tile(2 * P, BF16, "e%d_%d" % (j, u))
-                nc.vector.scalar_tensor_tensor(
-                    e[:].rearrange("p (s r) -> p s r", r=2),
-                    ub_turned[j][:].rearrange("p (r s) -> p s r", r=PACK)[:, :, 2 * u : 2 * u + 2],
-                    cf_sq[:, j : j + 1],
-                    va[j][:].rearrange("p (s r) -> p s r", r=PACK)[:, :, 2 * u : 2 * u + 2],
-                    MULT,
-                    ADD,
-                )
-                nc.tensor.transpose(turned[:, u * P : (u + 1) * P], e[:].bitcast(F32), ident[:])
-            weave_pairs(e_dst[j], turned)
-
-        def residual_on_tensor(j):
+        def fit_dealt(j):
             fitted = tile(N, F32, "fitted%d" % j)
-            nc.scalar.activation(fitted[:], ub_turned[j][:], COPY, scale=cf_sq[:, j : j + 1])
-            total = bank("a", j, "e_sum%d" % j)
+            nc.vector.scalar_tensor_tensor(
+                fitted[:].rearrange("p (r s) -> p r s", r=PACK),
+                u_ps[j][:].rearrange("p (s r) -> p r s", r=PACK),
+                cf_sq[j][:],
+                b_dealt[:].rearrange("p (r s) -> p r s", r=PACK),
+                MULT,
+                MULT,
+            )
+            sums[j] = bank("e", j, "e_sum%d" % j)
             for r in range(PACK):
                 cols = slice(r * P, (r + 1) * P)
-                nc.tensor.matmul(total[:, cols], fitted[:, cols], ident[:], start=True, stop=False, is_transpose=True)
-                nc.tensor.matmul(total[:, cols], va[j][:, r:N:PACK], ident[:], start=False, stop=True, is_transpose=True)
+                nc.tensor.matmul(sums[j][:, cols], fitted[:, cols], ident[:], start=r == 0, stop=False, is_transpose=True)
+
+        def gather_values(j, va):
+            nc.vector.tensor_tensor(va[:], v_win[j][:].indirect(offsets[:]), a_all[:], MULT)
+            dealt = tile(N, F32, "dealt%d" % j, tag="w_raw" if j == 0 else None)
+            nc.scalar.activation(
+                dealt[:].rearrange("p (r s) -> p s r", r=PACK),
+                va[:].rearrange("p (s r) -> p s r", r=PACK),
+                COPY,
+                scale=cf_neg[:, j : j + 1],
+            )
+            return dealt
+
+        def residual(j, dealt):
+            for r in range(PACK):
+                cols = slice(r * P, (r + 1) * P)
+                nc.tensor.matmul(sums[j][:, cols], dealt[:, cols], ident[:], start=False, stop=r == PACK - 1, is_transpose=True)
             nc.scalar.copy(
-                e_dst[j].rearrange("s (m r) -> s m r", r=PACK), total[:].rearrange("s (r m) -> s m r", r=PACK)
+                e_dst[j].rearrange("s (m r) -> s m r", r=PACK), sums[j][:].rearrange("s (r m) -> s m r", r=PACK)
             )
 
-        gather_values(0)
-        quantize_turned_keys(0)
-        residual_on_tensor(0)
-        gather_values(1)
-        quantize_turned_keys(1)
-        residual_on_tensor(1)
-        for j in range(2, TILES):
-            gather_values(j)
-            residual_on_vector(j)
+        dealt0 = gather_values(0, placed(N, F32, "va0", 12))
+        fit_dealt(0)
+        residual(0, dealt0)
+        dealt1 = gather_values(1, placed(N, F32, "va1", 2))
+        fit_dealt(1)
+        residual(1, dealt1)
+        fit_dealt(2)
+        residual(2, gather_values(2, tile(N, F32, "va2", tag="cf_sq1")))
 
-        e_codes = tile(N, U32, "e_codes", tag="va3")
-        e_scales = tile(N, U8, "e_scales")
-        start = 0
-        for part in e_turned:
+        j = TILES - 1
+        fitted = tile(N, F32, "fitted%d" % j)
+        nc.vector.scalar_tensor_tensor(fitted[:], u_ps[j][:], cf_sq[j][:], b_all[:], MULT, MULT)
+        halves = [slice(0, HALF), slice(HALF, N)]
+        va_both = tile(N, F32, "va_last", tag="cf_sq2")
+        va_last = [va_both[:, :HALF], va_both[:, HALF:]]
+        for h, slots in enumerate(halves):
+            part = offsets[:, slots.start // 16 : slots.stop // 16]
+            nc.vector.tensor_tensor(va_last[h], v_win[j][:].indirect(part), a_all[:, slots], MULT)
+        e_last = tile(N, BF16, "e_last")
+        for h, slots in enumerate(halves):
+            nc.vector.scalar_tensor_tensor(
+                e_last[:, slots], va_last[h], cf_neg[:, j : j + 1], fitted[:, slots], MULT, ADD
+            )
+        turned = bank("e", j, "e_turn")
+        turn_pairs(e_last[:], turned)
+        weave_pairs(e_dst[j], turned)
+
+        e_codes = tile(P + N, U32, "e_codes")
+        e_scales = tile(P + N, U8, "e_scales", tag="v_win3")
+        nc.gpsimd.memset(e_codes[:, :P], 0)
+        nc.gpsimd.memset(e_scales[:, :P], 0)
+        start = P
+        for part in e_in:
             cols = slice(start, start + part.shape[1] // PACK)
             nc.vector.quantize_mx(e_codes[:, cols].bitcast(E5M2), e_scales[:, cols], part[:])
             start = cols.stop
 
+        quantize_turned_keys(PACK - 1, tile(P, U8, "ki_scales3", tag="a_all"))
         out_rows = out.rearrange("(p t) f -> t p f", t=PACK)
-        for t in range(PACK):
-            o_ps = bank("b", t, "o_ps%d" % t)
-            cols = slice((t % 2) * P, (t % 2 + 1) * P)
+
+        def product(t, o_ps, window):
             nc.tensor.matmul_mx(
-                out=o_ps[:], lhsT=ki_codes[t // 2][:, cols].bitcast(E4M3), lhsT_scale=ki_scales[t // 2][:, cols],
-                rhs=e_codes[:].bitcast(E5M2), rhs_scale=e_scales[:], start=True, stop=True,
+                out=o_ps[:], lhsT=ki_codes[t][:].bitcast(E4M3), lhsT_scale=ki_scales[t][:],
+                rhs=e_codes[:, window].bitcast(E5M2), rhs_scale=e_scales[:, window], start=True, stop=True,
             )
-            for h, cols in enumerate([slice(0, N // 2), slice(N // 2, N)] if t == 0 else [slice(0, N)]):
-                o_sb = tile(cols.stop - cols.start, F32, "o_sb%d_%d" % (t, h))
-                if t % 2 == 0:
-                    nc.scalar.copy(o_sb[:], o_ps[:, cols])
-                else:
-                    nc.vector.tensor_copy(o_sb[:], o_ps[:, cols])
-                nc.sync.dma_start(out_rows[t][:, cols], o_sb[:])
+
+        for h, t in enumerate(EARLY_PLANES):
+            o_ps = bank("a", h, "early_ps%d" % t)
+            product(t, o_ps, slice(0, N))
+            o_sb = tile(N - P, F32, "early_sb%d" % t)
+            nc.scalar.copy(o_sb[:], o_ps[:, P:])
+            nc.sync.dma_start(out_rows[t][:, : N - P], o_sb[:])
+        final_banks = [("a", 2), ("a", 3), ("e", 0), ("e", 1)]
+        for t in range(PACK):
+            o_ps = bank(final_banks[t][0], final_banks[t][1], "o_ps%d" % t)
+            product(t, o_ps, slice(P, P + N))
+            cols = slice(N - P, N) if t in EARLY_PLANES else slice(0, N)
+            o_sb = tile(cols.stop - cols.start, F32, "o_sb%d" % t)
+            if t % 2 == 0:
+                nc.vector.tensor_copy(o_sb[:], o_ps[:, cols])
+            else:
+                nc.scalar.copy(o_sb[:], o_ps[:, cols])
+            nc.sync.dma_start(out_rows[t][:, cols], o_sb[:])

@@ -135,13 +135,18 @@ def tile_attend_gttt_W_kernel(tc, kT, vT, W, ts, tk, cf, offs, out):
         for j in range(TILES):
             nc.scalar.activation(cf_sq[j][:], cf_neg[:, j : j + 1], COPY, scale=cf_neg[:, j : j + 1])
 
-        a_all_ps = bank("a", 2, "a_all_ps")
-        b_all_ps = bank("a", 3, "b_all_ps")
+        a_all_ps = bank("e", 0, "a_all_ps")
+        b_all_ps = bank("e", 1, "b_all_ps")
         for col, spread in ((a_col, a_all_ps), (b_col, b_all_ps)):
             for c in range(TILES):
                 nc.tensor.transpose(spread[:, c * P : (c + 1) * P], col[:, c : c + 1].to_broadcast([P, P]), ident[:])
-        a_all = tile(N, F32, "a_all")
-        nc.scalar.copy(a_all[:], a_all_ps[:])
+        cf_a = []
+
+        def value_factor(j, dst):
+            cf_a.append(dst)
+            nc.scalar.activation(dst, a_all_ps[:], COPY, scale=cf_neg[:, j : j + 1])
+
+        value_factor(0, tile(N, F32, "cf_a0")[:])
 
         gather_keys(2)
 
@@ -149,8 +154,7 @@ def tile_attend_gttt_W_kernel(tc, kT, vT, W, ts, tk, cf, offs, out):
         nc.scalar.copy(
             b_dealt[:].rearrange("p (r s) -> p r s", r=PACK), b_all_ps[:].rearrange("p (s r) -> p r s", r=PACK)
         )
-        b_all = tile(N, F32, "b_all")
-        nc.scalar.copy(b_all[:], b_all_ps[:])
+        value_factor(1, tile(N, F32, "cf_a1")[:])
 
         last_turn = gather_keys(3)
 
@@ -165,6 +169,7 @@ def tile_attend_gttt_W_kernel(tc, kT, vT, W, ts, tk, cf, offs, out):
 
         w_planes = w_raw[:].rearrange("p (t f) -> p t f", t=PACK)
         u_ps = []
+        w_quantised = []
         for j in range(TILES):
             w_in = placed(N, BF16, "w_in%d" % j, (8, 2, 0, 4)[j] + 4)[:]
             dst, src = interleaved(w_in, w_planes[:, :, j * P : (j + 1) * P])
@@ -172,12 +177,19 @@ def tile_attend_gttt_W_kernel(tc, kT, vT, W, ts, tk, cf, offs, out):
             w_codes = tile(P, U32, "w_codes%d" % j)
             w_scales = tile(P, U8, "w_scales%d" % j)
             nc.vector.quantize_mx(w_codes[:].bitcast(E4M3), w_scales[:], w_in)
+            w_quantised.append((w_codes, w_scales))
+        late = tile(3 * N, F32, "late", tag="w_raw")
+        for j in range(2, TILES):
+            value_factor(j, late[:, (j - 2) * N : (j - 1) * N])
+        b_all = late[:, 2 * N :]
+        nc.scalar.copy(b_all, b_all_ps[:])
+        weave_pairs(k_turned[PACK - 1], last_turn)
+        for j, (w_codes, w_scales) in enumerate(w_quantised):
             u_ps.append(bank("a", j, "u_ps%d" % j))
             nc.tensor.matmul_mx(
                 out=u_ps[j][:], lhsT=w_codes[:].bitcast(E4M3), lhsT_scale=w_scales[:],
                 rhs=kd_codes[:].bitcast(E4M3), rhs_scale=kd_scales[:], start=True, stop=True,
             )
-        weave_pairs(k_turned[PACK - 1], last_turn)
 
         e_in = [tile(2 * N, BF16, "e_in01"), tile(N, BF16, "e_in2"), tile(N, BF16, "e_in3")]
         e_dst = [e_in[0][:, :N], e_in[0][:, N:], e_in[1][:], e_in[2][:]]
@@ -199,20 +211,13 @@ def tile_attend_gttt_W_kernel(tc, kT, vT, W, ts, tk, cf, offs, out):
                 nc.tensor.matmul(sums[j][:, cols], fitted[:, cols], ident[:], start=r == 0, stop=False, is_transpose=True)
 
         def gather_values(j, va):
-            nc.vector.tensor_tensor(va[:], v_win[j][:].indirect(offsets[:]), a_all[:], MULT)
-            dealt = tile(N, F32, "dealt%d" % j, tag="w_raw" if j == 0 else None)
-            nc.scalar.activation(
-                dealt[:].rearrange("p (r s) -> p s r", r=PACK),
-                va[:].rearrange("p (s r) -> p s r", r=PACK),
-                COPY,
-                scale=cf_neg[:, j : j + 1],
-            )
-            return dealt
+            nc.vector.tensor_tensor(va[:], v_win[j][:].indirect(offsets[:]), cf_a[j], MULT)
+            return va
 
         def residual(j, dealt):
             for r in range(PACK):
                 cols = slice(r * P, (r + 1) * P)
-                nc.tensor.matmul(sums[j][:, cols], dealt[:, cols], ident[:], start=False, stop=r == PACK - 1, is_transpose=True)
+                nc.tensor.matmul(sums[j][:, cols], dealt[:, r:N:PACK], ident[:], start=False, stop=r == PACK - 1, is_transpose=True)
             nc.scalar.copy(
                 e_dst[j].rearrange("s (m r) -> s m r", r=PACK), sums[j][:].rearrange("s (r m) -> s m r", r=PACK)
             )
@@ -228,18 +233,16 @@ def tile_attend_gttt_W_kernel(tc, kT, vT, W, ts, tk, cf, offs, out):
 
         j = TILES - 1
         fitted = tile(N, F32, "fitted%d" % j)
-        nc.vector.scalar_tensor_tensor(fitted[:], u_ps[j][:], cf_sq[j][:], b_all[:], MULT, MULT)
+        nc.vector.scalar_tensor_tensor(fitted[:], u_ps[j][:], cf_sq[j][:], b_all, MULT, MULT)
         halves = [slice(0, HALF), slice(HALF, N)]
         va_both = tile(N, F32, "va_last", tag="cf_sq2")
         va_last = [va_both[:, :HALF], va_both[:, HALF:]]
         for h, slots in enumerate(halves):
             part = offsets[:, slots.start // 16 : slots.stop // 16]
-            nc.vector.tensor_tensor(va_last[h], v_win[j][:].indirect(part), a_all[:, slots], MULT)
+            nc.vector.tensor_tensor(va_last[h], v_win[j][:].indirect(part), cf_a[j][:, slots], MULT)
         e_last = tile(N, BF16, "e_last")
         for h, slots in enumerate(halves):
-            nc.vector.scalar_tensor_tensor(
-                e_last[:, slots], va_last[h], cf_neg[:, j : j + 1], fitted[:, slots], MULT, ADD
-            )
+            nc.vector.tensor_tensor(e_last[:, slots], va_last[h], fitted[:, slots], ADD)
         turned = bank("e", j, "e_turn")
         turn_pairs(e_last[:], turned)
         weave_pairs(e_dst[j], turned)
@@ -247,14 +250,14 @@ def tile_attend_gttt_W_kernel(tc, kT, vT, W, ts, tk, cf, offs, out):
         e_codes = tile(P + N, U32, "e_codes")
         e_scales = tile(P + N, U8, "e_scales", tag="v_win3")
         nc.gpsimd.memset(e_codes[:, :P], 0)
-        nc.gpsimd.memset(e_scales[:, :P], 0)
+        nc.gpsimd.memset(e_scales[:, :P].bitcast(U32), 0)
         start = P
         for part in e_in:
             cols = slice(start, start + part.shape[1] // PACK)
             nc.vector.quantize_mx(e_codes[:, cols].bitcast(E5M2), e_scales[:, cols], part[:])
             start = cols.stop
 
-        quantize_turned_keys(PACK - 1, tile(P, U8, "ki_scales3", tag="a_all"))
+        quantize_turned_keys(PACK - 1, tile(P, U8, "ki_scales3", tag="w_raw"))
         out_rows = out.rearrange("(p t) f -> t p f", t=PACK)
 
         def product(t, o_ps, window):

@@ -11,7 +11,6 @@ TILES = N // P
 HALF = N // 2
 VECTOR_SLOTS = 336
 LAST = P - 1
-EARLY_PLANES = (2, 3)
 
 FLOPS = 2 * 2 * N * N * N
 BYTES = 4 * (2 * N * T + 2 * N * N + 2 * T + N) + 2 * P * (N // 16)
@@ -191,9 +190,16 @@ def tile_attend_gttt_W_kernel(tc, kT, vT, W, ts, tk, cf, offs, out):
                 rhs=kd_codes[:].bitcast(E4M3), rhs_scale=kd_scales[:], start=True, stop=True,
             )
 
-        e_in = [tile(2 * N, BF16, "e_in01"), tile(N, BF16, "e_in2"), tile(N, BF16, "e_in3")]
-        e_dst = [e_in[0][:, :N], e_in[0][:, N:], e_in[1][:], e_in[2][:]]
+        e_in = [tile(N, BF16, "e_in%d" % j) for j in range(TILES)]
+        e_dst = [part[:] for part in e_in]
         sums = {}
+
+        def quantize_e(part, name, tag):
+            width = part.shape[1] // PACK
+            codes = tile(width, U32, "e_codes" + name)
+            scales = tile(width, U8, "e_scales" + name, tag=tag)
+            nc.vector.quantize_mx(codes[:].bitcast(E5M2), scales[:], part[:])
+            return codes, scales
 
         def fit_dealt(j):
             fitted = tile(N, F32, "fitted%d" % j)
@@ -222,6 +228,29 @@ def tile_attend_gttt_W_kernel(tc, kT, vT, W, ts, tk, cf, offs, out):
                 e_dst[j].rearrange("s (m r) -> s m r", r=PACK), sums[j][:].rearrange("s (r m) -> s m r", r=PACK)
             )
 
+        out_rows = out.rearrange("(p t) f -> p t f", t=PACK)
+
+        def products(o_ps, planes, codes, scales):
+            width = codes.shape[1]
+            for n, t in enumerate(planes):
+                nc.tensor.matmul_mx(
+                    out=o_ps[:, n * width : (n + 1) * width], lhsT=ki_codes[t][:].bitcast(E4M3), lhsT_scale=ki_scales[t][:],
+                    rhs=codes[:].bitcast(E5M2), rhs_scale=scales[:], start=True, stop=True,
+                )
+
+        def store(o_ps, planes, cols, name, copy, queue):
+            width = (cols.stop - cols.start) * len(planes)
+            o_sb = tile(width, F32, name)
+            copy(o_sb[:], o_ps[:, :width])
+            queue.dma_start(
+                out_rows[:, planes[0] : planes[-1] + 1, cols], o_sb[:].rearrange("p (t f) -> p t f", t=len(planes))
+            )
+
+        def finish(j, quantised, group, copy):
+            o_ps = bank(group[0], group[1], "o%d_ps" % j)
+            products(o_ps, range(PACK), quantised[0], quantised[1])
+            store(o_ps, range(PACK), slice(j * P, (j + 1) * P), "o%d_sb" % j, copy, nc.sync)
+
         dealt0 = gather_values(0, placed(N, F32, "va0", 12))
         fit_dealt(0)
         residual(0, dealt0)
@@ -229,11 +258,13 @@ def tile_attend_gttt_W_kernel(tc, kT, vT, W, ts, tk, cf, offs, out):
         fit_dealt(1)
         residual(1, dealt1)
         fit_dealt(2)
+        quantize_turned_keys(PACK - 1, tile(P, U8, "ki_scales3", tag="v_win1"))
         residual(2, gather_values(2, tile(N, F32, "va2", tag="cf_sq1")))
 
         j = TILES - 1
         fitted = tile(N, F32, "fitted%d" % j)
         nc.vector.scalar_tensor_tensor(fitted[:], u_ps[j][:], cf_sq[j][:], b_all, MULT, MULT)
+        finish(0, quantize_e(e_in[0], "0", "cf_sq3"), ("a", 0), nc.scalar.copy)
         halves = [slice(0, HALF), slice(HALF, N)]
         va_both = tile(N, F32, "va_last", tag="cf_sq2")
         va_last = [va_both[:, :HALF], va_both[:, HALF:]]
@@ -247,39 +278,12 @@ def tile_attend_gttt_W_kernel(tc, kT, vT, W, ts, tk, cf, offs, out):
         turn_pairs(e_last[:], turned)
         weave_pairs(e_dst[j], turned)
 
-        e_codes = tile(P + N, U32, "e_codes")
-        e_scales = tile(P + N, U8, "e_scales", tag="v_win3")
-        nc.gpsimd.memset(e_codes[:, :P], 0)
-        nc.gpsimd.memset(e_scales[:, :P].bitcast(U32), 0)
-        start = P
-        for part in e_in:
-            cols = slice(start, start + part.shape[1] // PACK)
-            nc.vector.quantize_mx(e_codes[:, cols].bitcast(E5M2), e_scales[:, cols], part[:])
-            start = cols.stop
-
-        quantize_turned_keys(PACK - 1, tile(P, U8, "ki_scales3", tag="w_raw"))
-        out_rows = out.rearrange("(p t) f -> t p f", t=PACK)
-
-        def product(t, o_ps, window):
-            nc.tensor.matmul_mx(
-                out=o_ps[:], lhsT=ki_codes[t][:].bitcast(E4M3), lhsT_scale=ki_scales[t][:],
-                rhs=e_codes[:, window].bitcast(E5M2), rhs_scale=e_scales[:, window], start=True, stop=True,
-            )
-
-        for h, t in enumerate(EARLY_PLANES):
-            o_ps = bank("a", h, "early_ps%d" % t)
-            product(t, o_ps, slice(0, N))
-            o_sb = tile(N - P, F32, "early_sb%d" % t)
-            nc.scalar.copy(o_sb[:], o_ps[:, P:])
-            nc.sync.dma_start(out_rows[t][:, : N - P], o_sb[:])
-        final_banks = [("a", 2), ("a", 3), ("e", 0), ("e", 1)]
-        for t in range(PACK):
-            o_ps = bank(final_banks[t][0], final_banks[t][1], "o_ps%d" % t)
-            product(t, o_ps, slice(P, P + N))
-            cols = slice(N - P, N) if t in EARLY_PLANES else slice(0, N)
-            o_sb = tile(cols.stop - cols.start, F32, "o_sb%d" % t)
-            if t % 2 == 0:
-                nc.vector.tensor_copy(o_sb[:], o_ps[:, cols])
-            else:
-                nc.scalar.copy(o_sb[:], o_ps[:, cols])
-            nc.sync.dma_start(out_rows[t][:, cols], o_sb[:])
+        e1 = quantize_e(e_in[1], "1", "v_win3")
+        e2 = quantize_e(e_in[2], "2", "cf_sq2")
+        codes, scales = quantize_e(e_in[3], "3", "e_scales3")
+        finish(1, e1, ("a", 1), nc.vector.tensor_copy)
+        finish(2, e2, ("a", 2), nc.scalar.copy)
+        for h, (group, copy) in enumerate(((("a", 3), nc.vector.tensor_copy), (("e", 0), nc.scalar.copy))):
+            o_ps = bank(group[0], group[1], "o3_ps%d" % h)
+            products(o_ps, (2 * h, 2 * h + 1), codes, scales)
+            store(o_ps, (2 * h, 2 * h + 1), slice(3 * P, N), "o3_sb%d" % h, copy, nc.sync)

@@ -9,7 +9,9 @@ N = 512
 T = 2048
 TILES = N // P
 HALF = N // 2
-VECTOR_SLOTS = 336
+WEAVE_SLOTS = 128
+KEY_SLOTS = 192
+VALUE_SLOTS = 256
 LAST = P - 1
 
 FLOPS = 2 * 2 * N * N * N
@@ -25,6 +27,7 @@ E5M2 = mybir.dt.float8_e5m2_x4
 MULT = mybir.AluOpType.mult
 ADD = mybir.AluOpType.add
 COPY = mybir.ActivationFunctionType.Copy
+SQUARE = mybir.ActivationFunctionType.Square
 
 
 def interleaved(grouped, planes):
@@ -41,7 +44,7 @@ def tile_attend_gttt_W_kernel(tc, kT, vT, W, ts, tk, cf, offs, out):
         ps = ctx.enter_context(tc.psum_pool(name="ps", bufs=1))
 
         def placed(cols, dtype, name, at):
-            return reuse.tile([P, cols], dtype, name=name, align_bytes=64, offset=512 * at)
+            return reuse.tile([P, cols], dtype, name=name, align_bytes=64, offset=int(512 * at))
 
         def bank(group, j, name):
             return ps.tile([P, N], F32, name=name, tag="bank_%s%d" % (group, j))
@@ -50,12 +53,12 @@ def tile_attend_gttt_W_kernel(tc, kT, vT, W, ts, tk, cf, offs, out):
             return sb.tile([P, cols], dtype, name=name, tag=tag or name, align_bytes=64)
 
         offsets = sb.tile([P, N // 16], U16, name="offsets")
-        nc.sync.dma_start(offsets[:], offs)
 
-        k_rows = kT.rearrange("(p t) n -> t p n", t=PACK)
-        k_win = [tile(T, F32, "k_win%d" % t) for t in range(PACK)]
-        v_win = [tile(T, F32, "v_win%d" % j) for j in range(TILES)]
-        w_raw = tile(PACK * N, F32, "w_raw")
+        def listed(window, slots):
+            return window[:].indirect(offsets[:, slots.start // 16 : slots.stop // 16])
+
+        nc.sync.dma_start(offsets[:], offs)
+        every = slice(0, N)
         tk_win = tile(T, F32, "tk_win")
         ts_win = tile(T, F32, "ts_win")
         cf_rows = tile(P, F32, "cf_rows")
@@ -68,11 +71,16 @@ def tile_attend_gttt_W_kernel(tc, kT, vT, W, ts, tk, cf, offs, out):
         nc.scalar.dma_start(tk_win[LAST:, :], tk[0:1, :])
         nc.scalar.dma_start(ts_win[LAST:, :], ts[0:1, :])
         nc.scalar.dma_start(cf_rows[P - TILES :, :], cf.rearrange("(j p) o -> j (p o)", p=P))
-        for t in range(PACK):
+
+        k_rows = kT.rearrange("(p t) n -> t p n", t=PACK)
+        k_win = []
+
+        def load_keys(t):
+            k_win.append(tile(T, F32, "k_win%d" % t))
             nc.sync.dma_start(k_win[t][:], k_rows[t])
-        nc.sync.dma_start(w_raw[:], W.rearrange("(p t) f -> p (t f)", t=PACK))
-        for j in range(TILES):
-            nc.sync.dma_start(v_win[j][:], vT[j * P : (j + 1) * P, :])
+
+        for t in range(PACK):
+            load_keys(t)
 
         def turn_pairs(src, turned):
             words = src.bitcast(F32)
@@ -81,7 +89,7 @@ def tile_attend_gttt_W_kernel(tc, kT, vT, W, ts, tk, cf, offs, out):
 
         def turn_row(row, turned):
             for c in range(TILES):
-                nc.tensor.transpose(turned[:, c * P : (c + 1) * P], row[:, c * P : (c + 1) * P], ident[:])
+                nc.tensor.transpose(turned[:, c * P : (c + 1) * P], row[:, c:N:PACK], ident[:])
 
         def weave_pairs(dst, turned):
             nc.scalar.copy(
@@ -89,201 +97,233 @@ def tile_attend_gttt_W_kernel(tc, kT, vT, W, ts, tk, cf, offs, out):
                 turned[:, : 2 * P].rearrange("s (u m) -> s m u", u=2),
             )
 
-        k_planes = placed(PACK * N, BF16, "k_planes", 5)
-        k_turned = [k_planes[:, 2 * N : 3 * N], k_planes[:, 3 * N :], tile(N, BF16, "k_turned2")[:], placed(N, BF16, "k_turned3", 10)[:]]
-        ki_codes, ki_scales = [], []
+        k_planes = placed(PACK * N + KEY_SLOTS, BF16, "k_planes", 8)
+        k_turned = [k_planes[:, 2 * N : 3 * N], k_planes[:, 3 * N + KEY_SLOTS :], tile(N, BF16, "k_turned2")[:], tile(N, BF16, "k_turned3")[:]]
+        ki_codes = [tile(P, U32, "ki_codes%d" % t) for t in range(PACK)]
+        ki_scales = []
 
         def quantize_turned_keys(t, scales):
-            ki_codes.append(tile(P, U32, "ki_codes%d" % t))
             ki_scales.append(scales)
-            nc.vector.quantize_mx(ki_codes[t][:].bitcast(E4M3), ki_scales[t][:], k_turned[t])
+            nc.vector.quantize_mx(ki_codes[t][:].bitcast(E4M3), scales[:], k_turned[t])
+
+        def turn_keys(t, turned):
+            turn_pairs(k_planes[:, t * N : (t + 1) * N], turned)
+            weave_pairs(k_turned[t], turned)
 
         def gather_keys(t):
-            plane = k_planes[:, t * N : (t + 1) * N]
-            nc.vector.tensor_copy(plane, k_win[t][:].indirect(offsets[:]))
-            if t > 0:
-                quantize_turned_keys(t - 1, tile(P, U8, "ki_scales%d" % (t - 1), tag="k_win%d" % t))
-            turned = bank("e", t, "k_turn%d" % t)
-            turn_pairs(plane, turned)
-            if t < PACK - 1:
-                weave_pairs(k_turned[t], turned)
-            return turned
+            nc.vector.tensor_copy(k_planes[:, t * N : (t + 1) * N], listed(k_win[t], every))
+
+        def spread(col, name, group, j):
+            spread_ps = bank(group, j, name + "_ps")
+            for c in range(TILES):
+                nc.tensor.transpose(spread_ps[:, c * P : (c + 1) * P], col[:, c : c + 1].to_broadcast([P, P]), ident[:])
+            return spread_ps
+
+        def in_list_order(rows, dealt_ps, slots):
+            nc.scalar.copy(
+                rows[:].rearrange("p (s r) -> p s r", r=PACK),
+                dealt_ps[:].rearrange("p (r s) -> p s r", r=PACK)[:, slots.start // PACK : slots.stop // PACK],
+            )
 
         tk_row = tile(N, F32, "tk_row")
-        nc.vector.tensor_copy(tk_row[:], tk_win[:].indirect(offsets[:]))
+        nc.vector.tensor_copy(tk_row[:], listed(tk_win, every))
         tk_ps = bank("a", 0, "tk_ps")
         turn_row(tk_row, tk_ps)
+        tk_col = tile(TILES, F32, "tk_col")
+        nc.scalar.copy(tk_col[:], tk_ps[:, LAST:N:P])
         gather_keys(0)
+        w_raw = tile(PACK * N, F32, "w_raw")
+        nc.sync.dma_start(w_raw[:], W.rearrange("(p t) f -> p (t f)", t=PACK))
+        turn_keys(0, bank("e", 0, "k_turn0"))
+        tk_dealt = tile(N, F32, "tk_dealt")
+        nc.scalar.copy(tk_dealt[:], spread(tk_col, "tk_dealt", "a", 2)[:])
         a_row = tile(N, F32, "a_row")
-        nc.vector.tensor_tensor(a_row[:], ts_win[:].indirect(offsets[:]), tk_row[:], MULT)
+        nc.vector.tensor_tensor(a_row[:], listed(ts_win, every), tk_row[:], MULT)
         a_ps = bank("a", 1, "a_ps")
         turn_row(a_row, a_ps)
         a_col = tile(TILES, F32, "a_col")
         nc.scalar.copy(a_col[:], a_ps[:, LAST:N:P])
         b_col = tile(TILES, F32, "b_col")
         for c in range(TILES):
-            nc.scalar.activation(b_col[:, c : c + 1], tk_ps[:, c * P + LAST : (c + 1) * P], COPY, scale=a_col[:, c : c + 1])
+            nc.scalar.activation(b_col[:, c : c + 1], tk_col[:, c : c + 1], COPY, scale=a_col[:, c : c + 1])
 
+        v_win = []
+
+        def load_values(j):
+            v_win.append(tile(T, F32, "v_win%d" % j))
+            nc.sync.dma_start(v_win[j][:], vT[j * P : (j + 1) * P, :])
+
+        load_values(0)
         gather_keys(1)
+        load_values(1)
+        quantize_turned_keys(0, tile(P, U8, "ki_scales0"))
+        turn_keys(1, bank("e", 1, "k_turn1"))
 
-        cf_ps = bank("e", 3, "cf_ps")
+        cf_ps = bank("a", 0, "cf_ps")
         nc.tensor.transpose(cf_ps[:, :P], cf_rows[:], ident[:])
         cf_neg = tile(TILES, F32, "cf_neg")
         nc.scalar.activation(cf_neg[:], cf_ps[:, P - TILES : P], COPY, scale=-1.0)
-        cf_sq = [tile(1, F32, "cf_sq%d" % j) for j in range(TILES)]
-        for j in range(TILES):
-            nc.scalar.activation(cf_sq[j][:], cf_neg[:, j : j + 1], COPY, scale=cf_neg[:, j : j + 1])
+        cf_sq = tile(TILES, F32, "cf_sq")
+        nc.scalar.activation(cf_sq[:], cf_ps[:, P - TILES : P], SQUARE)
 
-        a_all_ps = bank("e", 0, "a_all_ps")
-        b_all_ps = bank("e", 1, "b_all_ps")
-        for col, spread in ((a_col, a_all_ps), (b_col, b_all_ps)):
-            for c in range(TILES):
-                nc.tensor.transpose(spread[:, c * P : (c + 1) * P], col[:, c : c + 1].to_broadcast([P, P]), ident[:])
-        cf_a = []
-
-        def value_factor(j, dst):
-            cf_a.append(dst)
-            nc.scalar.activation(dst, a_all_ps[:], COPY, scale=cf_neg[:, j : j + 1])
-
-        value_factor(0, tile(N, F32, "cf_a0")[:])
+        a_all_ps = spread(a_col, "a_all", "e", 2)
+        b_all_ps = spread(b_col, "b_all", "e", 3)
 
         gather_keys(2)
+        load_values(2)
+        quantize_turned_keys(1, tile(P, U8, "ki_scales1", tag="k_win2"))
+        turn_keys(2, bank("e", 0, "k_turn2"))
 
-        b_dealt = tile(N, F32, "b_dealt")
-        nc.scalar.copy(
-            b_dealt[:].rearrange("p (r s) -> p r s", r=PACK), b_all_ps[:].rearrange("p (s r) -> p r s", r=PACK)
-        )
-        value_factor(1, tile(N, F32, "cf_a1")[:])
+        last = PACK - 1
+        plane = k_planes[:, last * N : PACK * N]
+        nc.vector.tensor_copy(plane[:, KEY_SLOTS:], listed(k_win[last], slice(KEY_SLOTS, N)))
+        nc.scalar.activation(plane[:, :KEY_SLOTS], listed(k_win[last], slice(0, KEY_SLOTS)), COPY)
 
-        last_turn = gather_keys(3)
-
-        kd_in = tile(PACK * N, BF16, "kd_in")
-        dst, src = interleaved(kd_in[:], k_planes[:].rearrange("p (t n) -> p t n", t=PACK))
-        cut = VECTOR_SLOTS // 4
-        nc.vector.tensor_copy(dst[:, :cut], src[:, :cut])
-        nc.scalar.copy(dst[:, cut:], src[:, cut:])
+        planes = k_planes[:, : PACK * N].rearrange("p (t n) -> p t n", t=PACK)
+        kd_high = placed(PACK * (N - WEAVE_SLOTS), BF16, "kd_high", 25)
+        kd_low = placed(PACK * WEAVE_SLOTS, BF16, "kd_low", 22)
+        nc.vector.tensor_copy(*interleaved(kd_high[:], planes[:, :, WEAVE_SLOTS:]))
+        nc.scalar.copy(*interleaved(kd_low[:], planes[:, :, :WEAVE_SLOTS]))
+        turn_keys(last, bank("e", 1, "k_turn3"))
+        first, second = slice(0, P), slice(P, VALUE_SLOTS)
+        a_rest = placed(N - P, F32, "a_rest", 16.5)
+        in_list_order(a_rest, a_all_ps, slice(P, N))
         kd_codes = tile(N, U32, "kd_codes")
         kd_scales = tile(N, U8, "kd_scales")
-        nc.vector.quantize_mx(kd_codes[:].bitcast(E4M3), kd_scales[:], kd_in[:])
+        for part, slots in ((kd_low, slice(0, WEAVE_SLOTS)), (kd_high, slice(WEAVE_SLOTS, N))):
+            nc.vector.quantize_mx(kd_codes[:, slots].bitcast(E4M3), kd_scales[:, slots], part[:])
 
         w_planes = w_raw[:].rearrange("p (t f) -> p t f", t=PACK)
+        w_in = [placed(N, BF16, "w_in%d" % j, (20.5, 23, 8.5, 12.5)[j]) for j in range(TILES)]
         u_ps = []
-        w_quantised = []
-        for j in range(TILES):
-            w_in = placed(N, BF16, "w_in%d" % j, (8, 2, 0, 4)[j] + 4)[:]
-            dst, src = interleaved(w_in, w_planes[:, :, j * P : (j + 1) * P])
-            nc.scalar.copy(dst, src)
+
+        def lay_out(j, copy):
+            copy(*interleaved(w_in[j][:], w_planes[:, :, j * P : (j + 1) * P]))
+
+        def first_product(j):
             w_codes = tile(P, U32, "w_codes%d" % j)
             w_scales = tile(P, U8, "w_scales%d" % j)
-            nc.vector.quantize_mx(w_codes[:].bitcast(E4M3), w_scales[:], w_in)
-            w_quantised.append((w_codes, w_scales))
-        late = tile(3 * N, F32, "late", tag="w_raw")
-        for j in range(2, TILES):
-            value_factor(j, late[:, (j - 2) * N : (j - 1) * N])
-        b_all = late[:, 2 * N :]
-        nc.scalar.copy(b_all, b_all_ps[:])
-        weave_pairs(k_turned[PACK - 1], last_turn)
-        for j, (w_codes, w_scales) in enumerate(w_quantised):
+            nc.vector.quantize_mx(w_codes[:].bitcast(E4M3), w_scales[:], w_in[j][:])
             u_ps.append(bank("a", j, "u_ps%d" % j))
             nc.tensor.matmul_mx(
                 out=u_ps[j][:], lhsT=w_codes[:].bitcast(E4M3), lhsT_scale=w_scales[:],
                 rhs=kd_codes[:].bitcast(E4M3), rhs_scale=kd_scales[:], start=True, stop=True,
             )
 
-        e_in = [tile(N, BF16, "e_in%d" % j) for j in range(TILES)]
-        e_dst = [part[:] for part in e_in]
+        lay_out(0, nc.vector.tensor_copy)
+        lay_out(2, nc.scalar.copy)
+        lay_out(3, nc.scalar.copy)
+        quantize_turned_keys(2, placed(P, U8, "ki_scales2", 22.5))
+        first_product(0)
+        lay_out(1, nc.vector.tensor_copy)
+        load_values(3)
+        b_all = placed(N, F32, "b_all", 4.5)
+        in_list_order(b_all, b_all_ps, every)
+        quantize_turned_keys(last, tile(P, U8, "ki_scales3"))
+        a_first = {j: tile(P, F32, "a_first%d" % j, tag="k_turned%d" % j) for j in (2, 3)}
+        for j in (2, 3):
+            in_list_order(a_first[j], a_all_ps, first)
+        for j in range(1, TILES):
+            first_product(j)
+
+        fitted = [tile(N, F32, "fitted%d" % j) for j in range(TILES)]
+        e_rows = {j: tile(N, BF16, "e_rows%d" % j) for j in range(2, TILES)}
+        e_in = [tile(N, BF16, "e_in%d" % j, tag=tag) for j, tag in enumerate((None, "k_turned2", "v_win3", None))]
+        mine, theirs = slice(0, VALUE_SLOTS), slice(VALUE_SLOTS, N)
+
+        def fit(j):
+            nc.vector.scalar_tensor_tensor(fitted[j][:], u_ps[j][:], cf_sq[:, j : j + 1], b_all[:], MULT, MULT)
+
+        def residual(j, va, slots):
+            nc.vector.scalar_tensor_tensor(
+                e_rows[j][:, slots], va, cf_neg[:, j : j + 1], fitted[j][:, slots], MULT, ADD
+            )
+
+        turned = {j: bank("e", j, "e_turn%d" % j) for j in range(2, TILES)}
         sums = {}
 
-        def quantize_e(part, name, tag):
-            width = part.shape[1] // PACK
-            codes = tile(width, U32, "e_codes" + name)
-            scales = tile(width, U8, "e_scales" + name, tag=tag)
-            nc.vector.quantize_mx(codes[:].bitcast(E5M2), scales[:], part[:])
-            return codes, scales
-
         def fit_dealt(j):
-            fitted = tile(N, F32, "fitted%d" % j)
             nc.vector.scalar_tensor_tensor(
-                fitted[:].rearrange("p (r s) -> p r s", r=PACK),
+                fitted[j][:].rearrange("p (r s) -> p r s", r=PACK),
                 u_ps[j][:].rearrange("p (s r) -> p r s", r=PACK),
-                cf_sq[j][:],
-                b_dealt[:].rearrange("p (r s) -> p r s", r=PACK),
+                cf_sq[:, j : j + 1],
+                tk_dealt[:].rearrange("p (r s) -> p r s", r=PACK),
                 MULT,
                 MULT,
             )
             sums[j] = bank("e", j, "e_sum%d" % j)
             for r in range(PACK):
                 cols = slice(r * P, (r + 1) * P)
-                nc.tensor.matmul(sums[j][:, cols], fitted[:, cols], ident[:], start=r == 0, stop=False, is_transpose=True)
+                nc.tensor.matmul(sums[j][:, cols], fitted[j][:, cols], ident[:], start=r == 0, stop=False, is_transpose=True)
 
-        def gather_values(j, va):
-            nc.vector.tensor_tensor(va[:], v_win[j][:].indirect(offsets[:]), cf_a[j], MULT)
-            return va
-
-        def residual(j, dealt):
+        def added_tile(j):
+            raw = placed(N, F32, "raw%d" % j, 8.5 + 4 * j)
+            nc.scalar.activation(raw[:], listed(v_win[j], every), COPY, scale=cf_neg[:, j : j + 1])
             for r in range(PACK):
                 cols = slice(r * P, (r + 1) * P)
-                nc.tensor.matmul(sums[j][:, cols], dealt[:, r:N:PACK], ident[:], start=False, stop=r == PACK - 1, is_transpose=True)
-            nc.scalar.copy(
-                e_dst[j].rearrange("s (m r) -> s m r", r=PACK), sums[j][:].rearrange("s (r m) -> s m r", r=PACK)
+                nc.tensor.matmul(sums[j][:, cols], raw[:, r:N:PACK], ident[:], start=False, stop=r == PACK - 1, is_transpose=True)
+
+        def weigh(j):
+            nc.vector.tensor_tensor(
+                e_in[j][:].rearrange("s (m r) -> s m r", r=PACK),
+                sums[j][:].rearrange("s (r m) -> s m r", r=PACK),
+                a_col[:].unsqueeze(1).to_broadcast([P, P, PACK]),
+                MULT,
             )
+
+        def quantize_e(j, scales):
+            codes = tile(P, U32, "e_codes%d" % j)
+            nc.vector.quantize_mx(codes[:].bitcast(E5M2), scales[:], e_in[j][:])
+            return codes, scales
 
         out_rows = out.rearrange("(p t) f -> p t f", t=PACK)
 
-        def products(o_ps, planes, codes, scales):
-            width = codes.shape[1]
+        def finish(j, quantised, planes, o_ps, copy, name, tag):
+            codes, scales = quantised
             for n, t in enumerate(planes):
                 nc.tensor.matmul_mx(
-                    out=o_ps[:, n * width : (n + 1) * width], lhsT=ki_codes[t][:].bitcast(E4M3), lhsT_scale=ki_scales[t][:],
+                    out=o_ps[:, n * P : (n + 1) * P], lhsT=ki_codes[t][:].bitcast(E4M3), lhsT_scale=ki_scales[t][:],
                     rhs=codes[:].bitcast(E5M2), rhs_scale=scales[:], start=True, stop=True,
                 )
-
-        def store(o_ps, planes, cols, name, copy, queue):
-            width = (cols.stop - cols.start) * len(planes)
-            o_sb = tile(width, F32, name)
+            width = P * len(planes)
+            o_sb = tile(width, F32, name, tag=tag)
             copy(o_sb[:], o_ps[:, :width])
-            queue.dma_start(
-                out_rows[:, planes[0] : planes[-1] + 1, cols], o_sb[:].rearrange("p (t f) -> p t f", t=len(planes))
+            nc.sync.dma_start(
+                out_rows[:, planes[0] : planes[-1] + 1, j * P : (j + 1) * P],
+                o_sb[:].rearrange("p (t f) -> p t f", t=len(planes)),
             )
 
-        def finish(j, quantised, group, copy):
-            o_ps = bank(group[0], group[1], "o%d_ps" % j)
-            products(o_ps, range(PACK), quantised[0], quantised[1])
-            store(o_ps, range(PACK), slice(j * P, (j + 1) * P), "o%d_sb" % j, copy, nc.sync)
+        whole = range(PACK)
+        def shared_tile(j, between):
+            raw = tile(N - VALUE_SLOTS, F32, "raw%d" % j)
+            va = tile(N, F32, "va%d" % j)
+            nc.scalar.activation(raw[:], listed(v_win[j], theirs), COPY)
+            nc.vector.tensor_tensor(va[:, first], listed(v_win[j], first), a_first[j][:], MULT)
+            nc.vector.tensor_tensor(va[:, second], listed(v_win[j], second), a_rest[:, : VALUE_SLOTS - P], MULT)
+            made = between()
+            nc.vector.tensor_tensor(va[:, theirs], raw[:], a_rest[:, VALUE_SLOTS - P :], MULT)
+            residual(j, va[:, mine], mine)
+            residual(j, va[:, theirs], theirs)
+            return made, va
 
-        dealt0 = gather_values(0, placed(N, F32, "va0", 12))
         fit_dealt(0)
-        residual(0, dealt0)
-        dealt1 = gather_values(1, placed(N, F32, "va1", 2))
+        added_tile(0)
         fit_dealt(1)
-        residual(1, dealt1)
-        fit_dealt(2)
-        quantize_turned_keys(PACK - 1, tile(P, U8, "ki_scales3", tag="v_win1"))
-        residual(2, gather_values(2, tile(N, F32, "va2", tag="cf_sq1")))
-
+        fit(2)
+        fit(3)
+        added_tile(1)
+        weigh(0)
+        finish(0, quantize_e(0, tile(P, U8, "e_scales0")), whole, bank("a", 0, "o_ps0"), nc.scalar.copy, "o_sb0", "v_win2")
+        shared_tile(2, lambda: weigh(1))
+        turn_pairs(e_rows[2][:], turned[2])
         j = TILES - 1
-        fitted = tile(N, F32, "fitted%d" % j)
-        nc.vector.scalar_tensor_tensor(fitted[:], u_ps[j][:], cf_sq[j][:], b_all, MULT, MULT)
-        finish(0, quantize_e(e_in[0], "0", "cf_sq3"), ("a", 0), nc.scalar.copy)
-        halves = [slice(0, HALF), slice(HALF, N)]
-        va_both = tile(N, F32, "va_last", tag="cf_sq2")
-        va_last = [va_both[:, :HALF], va_both[:, HALF:]]
-        for h, slots in enumerate(halves):
-            part = offsets[:, slots.start // 16 : slots.stop // 16]
-            nc.vector.tensor_tensor(va_last[h], v_win[j][:].indirect(part), cf_a[j][:, slots], MULT)
-        e_last = tile(N, BF16, "e_last")
-        for h, slots in enumerate(halves):
-            nc.vector.tensor_tensor(e_last[:, slots], va_last[h], fitted[:, slots], ADD)
-        turned = bank("e", j, "e_turn")
-        turn_pairs(e_last[:], turned)
-        weave_pairs(e_dst[j], turned)
-
-        e1 = quantize_e(e_in[1], "1", "v_win3")
-        e2 = quantize_e(e_in[2], "2", "cf_sq2")
-        codes, scales = quantize_e(e_in[3], "3", "e_scales3")
-        finish(1, e1, ("a", 1), nc.vector.tensor_copy)
-        finish(2, e2, ("a", 2), nc.scalar.copy)
-        for h, (group, copy) in enumerate(((("a", 3), nc.vector.tensor_copy), (("e", 0), nc.scalar.copy))):
-            o_ps = bank(group[0], group[1], "o3_ps%d" % h)
-            products(o_ps, (2 * h, 2 * h + 1), codes, scales)
-            store(o_ps, (2 * h, 2 * h + 1), slice(3 * P, N), "o3_sb%d" % h, copy, nc.sync)
+        e1, va = shared_tile(j, lambda: quantize_e(1, tile(P, U8, "e_scales1", tag="k_turned3")))
+        weave_pairs(e_in[2][:], turned[2])
+        finish(1, e1, whole, bank("a", 1, "o_ps1"), nc.scalar.copy, "o_sb1", None)
+        turn_pairs(e_rows[j][:], turned[j])
+        e2 = quantize_e(2, tile(P, U8, "e_scales2", tag="va3"))
+        weave_pairs(e_in[j][:], turned[j])
+        e3 = quantize_e(j, tile(P, U8, "e_scales3"))
+        finish(2, e2, whole, bank("a", 2, "o_ps2"), nc.vector.tensor_copy, "o_sb2", "e_in3")
+        finish(j, e3, (0, 1), bank("a", 3, "o_ps3"), nc.vector.tensor_copy, "o_sb3", None)
+        finish(j, e3, (2, 3), bank("e", 0, "o_ps4"), nc.scalar.copy, "o_sb4", None)

@@ -226,7 +226,7 @@ def tile_attend_gttt_W_kernel(tc, kT, vT, W, ts, tk, cf, offs, out):
         for j in range(1, TILES):
             first_product(j)
 
-        fitted = [tile(N, F32, "fitted%d" % j) for j in range(TILES)]
+        fitted = [tile(N, F32, "fitted%d" % j, tag="v_win0" if j == 1 else None) for j in range(TILES)]
         e_rows = {j: tile(N, BF16, "e_rows%d" % j) for j in range(2, TILES)}
         e_in = [tile(N, BF16, "e_in%d" % j, tag=tag) for j, tag in enumerate((None, "k_turned2", "v_win3", None))]
         mine, theirs = slice(0, VALUE_SLOTS), slice(VALUE_SLOTS, N)
@@ -308,12 +308,12 @@ def tile_attend_gttt_W_kernel(tc, kT, vT, W, ts, tk, cf, offs, out):
 
         fit_dealt(0)
         added_tile(0)
-        fit_dealt(1)
         fit(2)
         fit(3)
+        fit_dealt(1)
         added_tile(1)
         weigh(0)
-        finish(0, quantize_e(0, tile(P, U8, "e_scales0")), whole, bank("a", 0, "o_ps0"), nc.scalar.copy, "o_sb0", "v_win2")
+        finish(0, quantize_e(0, tile(P, U8, "e_scales0", tag="v_win1")), whole, bank("a", 0, "o_ps0"), nc.scalar.copy, "o_sb0", "v_win2")
         shared_tile(2, lambda: weigh(1))
         turn_pairs(e_rows[2][:], turned[2])
         j = TILES - 1
@@ -324,6 +324,6 @@ def tile_attend_gttt_W_kernel(tc, kT, vT, W, ts, tk, cf, offs, out):
         e2 = quantize_e(2, tile(P, U8, "e_scales2", tag="va3"))
         weave_pairs(e_in[j][:], turned[j])
         e3 = quantize_e(j, tile(P, U8, "e_scales3"))
-        finish(2, e2, whole, bank("a", 2, "o_ps2"), nc.vector.tensor_copy, "o_sb2", "e_in3")
+        finish(2, e2, whole, bank("a", 2, "o_ps2"), nc.scalar.copy, "o_sb2", None)
         finish(j, e3, (0, 1), bank("a", 3, "o_ps3"), nc.vector.tensor_copy, "o_sb3", None)
         finish(j, e3, (2, 3), bank("e", 0, "o_ps4"), nc.scalar.copy, "o_sb4", None)

@@ -65,9 +65,9 @@ def tile_attend_gttt_W_kernel(tc, kT, vT, W, ts, tk, cf, offs, out):
         ident = tile(P, F32, "ident")
 
         nc.gpsimd.memset(cf_rows[: P - TILES, :], 0.0)
-        nc.vector.memset(tk_win[:LAST, :], 0.0)
+        nc.vector.memset(tk_win[:LAST, :].bitcast(U32), 0)
+        nc.vector.memset(ts_win[:LAST, :].bitcast(U32), 0)
         make_identity(nc, ident[:])
-        nc.gpsimd.memset(ts_win[:LAST, :], 0.0)
         nc.scalar.dma_start(tk_win[LAST:, :], tk[0:1, :])
         nc.scalar.dma_start(ts_win[LAST:, :], ts[0:1, :])
         nc.scalar.dma_start(cf_rows[P - TILES :, :], cf.rearrange("(j p) o -> j (p o)", p=P))

@@ -13,6 +13,7 @@ WEAVE_SLOTS = 128
 KEY_SLOTS = 192
 VALUE_SLOTS = 256
 LAST = P - 1
+TS_ROW = P // 2 - 1
 
 FLOPS = 2 * 2 * N * N * N
 BYTES = 4 * (2 * N * T + 2 * N * N + 2 * T + N) + 2 * P * (N // 16)
@@ -60,17 +61,17 @@ def tile_attend_gttt_W_kernel(tc, kT, vT, W, ts, tk, cf, offs, out):
         nc.sync.dma_start(offsets[:], offs)
         every = slice(0, N)
         tk_win = tile(T, F32, "tk_win")
-        ts_win = tile(T, F32, "ts_win")
+        ts_win = placed(T, F32, "ts_win", 60)
         cf_rows = tile(P, F32, "cf_rows")
         ident = tile(P, F32, "ident")
 
         nc.gpsimd.memset(cf_rows[: P - TILES, :], 0.0)
         nc.vector.memset(tk_win[:LAST, :].bitcast(U32), 0)
-        nc.vector.memset(ts_win[:LAST, :].bitcast(U32), 0)
+        nc.vector.memset(ts_win[:TS_ROW, :].bitcast(U32), 0)
         make_identity(nc, ident[:])
+        nc.gpsimd.memset(ts_win[TS_ROW + 1 :, :], 0.0)
         nc.scalar.dma_start(tk_win[LAST:, :], tk[0:1, :])
-        nc.scalar.dma_start(ts_win[LAST:, :], ts[0:1, :])
-        nc.scalar.dma_start(cf_rows[P - TILES :, :], cf.rearrange("(j p) o -> j (p o)", p=P))
+        nc.scalar.dma_start(ts_win[TS_ROW : TS_ROW + 1, :], ts[0:1, :])
 
         k_rows = kT.rearrange("(p t) n -> t p n", t=PACK)
         k_win = []
@@ -79,7 +80,9 @@ def tile_attend_gttt_W_kernel(tc, kT, vT, W, ts, tk, cf, offs, out):
             k_win.append(tile(T, F32, "k_win%d" % t))
             nc.sync.dma_start(k_win[t][:], k_rows[t])
 
-        for t in range(PACK):
+        load_keys(0)
+        nc.sync.dma_start(cf_rows[P - TILES :, :], cf.rearrange("(j p) o -> j (p o)", p=P))
+        for t in range(1, PACK):
             load_keys(t)
 
         def turn_pairs(src, turned):
@@ -98,7 +101,7 @@ def tile_attend_gttt_W_kernel(tc, kT, vT, W, ts, tk, cf, offs, out):
             )
 
         k_planes = placed(PACK * N + KEY_SLOTS, BF16, "k_planes", 8)
-        k_turned = [k_planes[:, 2 * N : 3 * N], k_planes[:, 3 * N + KEY_SLOTS :], tile(N, BF16, "k_turned2")[:], tile(N, BF16, "k_turned3")[:]]
+        k_turned = [placed(N, BF16, "k_turned0", 60)[:], k_planes[:, 3 * N + KEY_SLOTS :], tile(N, BF16, "k_turned2")[:], tile(N, BF16, "k_turned3")[:]]
         ki_codes = [tile(P, U32, "ki_codes%d" % t) for t in range(PACK)]
         ki_scales = []
 
@@ -126,23 +129,25 @@ def tile_attend_gttt_W_kernel(tc, kT, vT, W, ts, tk, cf, offs, out):
             )
 
         tk_row = tile(N, F32, "tk_row")
-        nc.vector.tensor_copy(tk_row[:], listed(tk_win, every))
+        nc.scalar.activation(tk_row[:], listed(tk_win, every), COPY)
+        ts_row = tile(N, F32, "ts_row")
+        nc.scalar.activation(ts_row[:], listed(ts_win, every), COPY)
         tk_ps = bank("a", 0, "tk_ps")
         turn_row(tk_row, tk_ps)
-        tk_col = tile(TILES, F32, "tk_col")
+        tk_col = placed(TILES, F32, "tk_col", 62)
         nc.scalar.copy(tk_col[:], tk_ps[:, LAST:N:P])
+        ts_ps = bank("a", 1, "ts_ps")
+        turn_row(ts_row, ts_ps)
         gather_keys(0)
         w_raw = tile(PACK * N, F32, "w_raw")
         nc.sync.dma_start(w_raw[:], W.rearrange("(p t) f -> p (t f)", t=PACK))
         turn_keys(0, bank("e", 0, "k_turn0"))
         tk_dealt = tile(N, F32, "tk_dealt")
         nc.scalar.copy(tk_dealt[:], spread(tk_col, "tk_dealt", "a", 2)[:])
-        a_row = tile(N, F32, "a_row")
-        nc.vector.tensor_tensor(a_row[:], listed(ts_win, every), tk_row[:], MULT)
-        a_ps = bank("a", 1, "a_ps")
-        turn_row(a_row, a_ps)
         a_col = tile(TILES, F32, "a_col")
-        nc.scalar.copy(a_col[:], a_ps[:, LAST:N:P])
+        for c in range(TILES):
+            at = c * P + TS_ROW
+            nc.scalar.activation(a_col[:, c : c + 1], ts_ps[:, at : at + 1], COPY, scale=tk_col[:, c : c + 1])
         b_col = tile(TILES, F32, "b_col")
         for c in range(TILES):
             nc.scalar.activation(b_col[:, c : c + 1], tk_col[:, c : c + 1], COPY, scale=a_col[:, c : c + 1])
@@ -156,7 +161,7 @@ def tile_attend_gttt_W_kernel(tc, kT, vT, W, ts, tk, cf, offs, out):
         load_values(0)
         gather_keys(1)
         load_values(1)
-        quantize_turned_keys(0, tile(P, U8, "ki_scales0"))
+        quantize_turned_keys(0, tile(P, U8, "ki_scales0", tag="k_win1"))
         turn_keys(1, bank("e", 1, "k_turn1"))
 
         cf_ps = bank("a", 0, "cf_ps")

@@ -11,7 +11,7 @@ TILES = N // P
 HALF = N // 2
 WEAVE_SLOTS = 128
 KEY_SLOTS = 192
-VALUE_SLOTS = 256
+VALUE_SLOTS = {2: 256, 3: 288}
 LAST = P - 1
 TS_ROW = P // 2 - 1
 
@@ -190,7 +190,7 @@ def tile_attend_gttt_W_kernel(tc, kT, vT, W, ts, tk, cf, offs, out):
         nc.vector.tensor_copy(*interleaved(kd_high[:], planes[:, :, WEAVE_SLOTS:]))
         nc.scalar.copy(*interleaved(kd_low[:], planes[:, :, :WEAVE_SLOTS]))
         turn_keys(last, bank("e", 1, "k_turn3"))
-        first, second = slice(0, P), slice(P, VALUE_SLOTS)
+        first = slice(0, P)
         a_rest = placed(N - P, F32, "a_rest", 16.5)
         in_list_order(a_rest, a_all_ps, slice(P, N))
         kd_codes = tile(N, U32, "kd_codes")
@@ -234,7 +234,6 @@ def tile_attend_gttt_W_kernel(tc, kT, vT, W, ts, tk, cf, offs, out):
         fitted = [tile(N, F32, "fitted%d" % j, tag="v_win0" if j == 1 else None) for j in range(TILES)]
         e_rows = {j: tile(N, BF16, "e_rows%d" % j) for j in range(2, TILES)}
         e_in = [tile(N, BF16, "e_in%d" % j, tag=tag) for j, tag in enumerate((None, "k_turned2", "v_win3", None))]
-        mine, theirs = slice(0, VALUE_SLOTS), slice(VALUE_SLOTS, N)
 
         def fit(j):
             nc.vector.scalar_tensor_tensor(fitted[j][:], u_ps[j][:], cf_sq[:, j : j + 1], b_all[:], MULT, MULT)
@@ -283,30 +282,38 @@ def tile_attend_gttt_W_kernel(tc, kT, vT, W, ts, tk, cf, offs, out):
 
         out_rows = out.rearrange("(p t) f -> p t f", t=PACK)
 
-        def finish(j, quantised, planes, o_ps, copy, name, tag):
+        def products(quantised, planes, o_ps):
             codes, scales = quantised
             for n, t in enumerate(planes):
                 nc.tensor.matmul_mx(
                     out=o_ps[:, n * P : (n + 1) * P], lhsT=ki_codes[t][:].bitcast(E4M3), lhsT_scale=ki_scales[t][:],
                     rhs=codes[:].bitcast(E5M2), rhs_scale=scales[:], start=True, stop=True,
                 )
-            width = P * len(planes)
-            o_sb = tile(width, F32, name, tag=tag)
-            copy(o_sb[:], o_ps[:, :width])
+
+        def store(j, planes, o_sb):
             nc.sync.dma_start(
                 out_rows[:, planes[0] : planes[-1] + 1, j * P : (j + 1) * P],
                 o_sb[:].rearrange("p (t f) -> p t f", t=len(planes)),
             )
 
+        def finish(j, quantised, planes, o_ps, copy, name, tag):
+            products(quantised, planes, o_ps)
+            width = P * len(planes)
+            o_sb = tile(width, F32, name, tag=tag)
+            copy(o_sb[:], o_ps[:, :width])
+            store(j, planes, o_sb)
+
         whole = range(PACK)
         def shared_tile(j, between):
-            raw = tile(N - VALUE_SLOTS, F32, "raw%d" % j)
+            cut = VALUE_SLOTS[j]
+            second, mine, theirs = slice(P, cut), slice(0, cut), slice(cut, N)
+            raw = tile(N - cut, F32, "raw%d" % j)
             va = tile(N, F32, "va%d" % j)
             nc.scalar.activation(raw[:], listed(v_win[j], theirs), COPY)
             nc.vector.tensor_tensor(va[:, first], listed(v_win[j], first), a_first[j][:], MULT)
-            nc.vector.tensor_tensor(va[:, second], listed(v_win[j], second), a_rest[:, : VALUE_SLOTS - P], MULT)
+            nc.vector.tensor_tensor(va[:, second], listed(v_win[j], second), a_rest[:, : cut - P], MULT)
             made = between()
-            nc.vector.tensor_tensor(va[:, theirs], raw[:], a_rest[:, VALUE_SLOTS - P :], MULT)
+            nc.vector.tensor_tensor(va[:, theirs], raw[:], a_rest[:, cut - P :], MULT)
             residual(j, va[:, mine], mine)
             residual(j, va[:, theirs], theirs)
             return made, va
@@ -329,6 +336,10 @@ def tile_attend_gttt_W_kernel(tc, kT, vT, W, ts, tk, cf, offs, out):
         e2 = quantize_e(2, tile(P, U8, "e_scales2", tag="va3"))
         weave_pairs(e_in[j][:], turned[j])
         e3 = quantize_e(j, tile(P, U8, "e_scales3"))
-        finish(2, e2, whole, bank("a", 2, "o_ps2"), nc.scalar.copy, "o_sb2", None)
+        o_sb = tile(N, F32, "o_sb2")
+        for h, o_ps in enumerate((bank("a", 2, "o_ps2"), bank("e", 1, "o_ps2b"))):
+            products(e2, (2 * h, 2 * h + 1), o_ps)
+            nc.scalar.copy(o_sb[:, h * HALF : (h + 1) * HALF], o_ps[:, :HALF])
+        store(2, whole, o_sb)
         finish(j, e3, (0, 1), bank("a", 3, "o_ps3"), nc.vector.tensor_copy, "o_sb3", None)
         finish(j, e3, (2, 3), bank("e", 0, "o_ps4"), nc.scalar.copy, "o_sb4", None)

@@ -101,7 +101,7 @@ def tile_attend_gttt_W_kernel(tc, kT, vT, W, ts, tk, cf, offs, out):
             )
 
         k_planes = placed(PACK * N + KEY_SLOTS, BF16, "k_planes", 8)
-        k_turned = [placed(N, BF16, "k_turned0", 60)[:], k_planes[:, 3 * N + KEY_SLOTS :], tile(N, BF16, "k_turned2")[:], tile(N, BF16, "k_turned3")[:]]
+        k_turned = [placed(N, BF16, "k_turned0", 60)[:], k_planes[:, 3 * N + KEY_SLOTS :], None, tile(N, BF16, "k_turned3")[:]]
         ki_codes = [tile(P, U32, "ki_codes%d" % t) for t in range(PACK)]
         ki_scales = []
 
@@ -173,26 +173,32 @@ def tile_attend_gttt_W_kernel(tc, kT, vT, W, ts, tk, cf, offs, out):
 
         a_all_ps = spread(a_col, "a_all", "e", 2)
         b_all_ps = spread(b_col, "b_all", "e", 3)
+        first = slice(0, P)
+        a_first = {j: tile(P, F32, "a_first%d" % j) for j in (2, 3)}
+        for j in (2, 3):
+            in_list_order(a_first[j], a_all_ps, first)
+        a_rest = tile(N - P, F32, "a_rest")
+        in_list_order(a_rest, a_all_ps, slice(P, N))
 
         gather_keys(2)
         load_values(2)
         quantize_turned_keys(1, tile(P, U8, "ki_scales1", tag="k_win2"))
-        turn_keys(2, bank("e", 0, "k_turn2"))
+        turned2 = bank("e", 2, "k_turn2")
+        turn_pairs(k_planes[:, 2 * N : 3 * N], turned2)
 
         last = PACK - 1
         plane = k_planes[:, last * N : PACK * N]
         nc.vector.tensor_copy(plane[:, KEY_SLOTS:], listed(k_win[last], slice(KEY_SLOTS, N)))
         nc.scalar.activation(plane[:, :KEY_SLOTS], listed(k_win[last], slice(0, KEY_SLOTS)), COPY)
 
+        k_turned[2] = tile(N, BF16, "k_turned2", tag="k_win3")[:]
+        weave_pairs(k_turned[2], turned2)
         planes = k_planes[:, : PACK * N].rearrange("p (t n) -> p t n", t=PACK)
         kd_high = placed(PACK * (N - WEAVE_SLOTS), BF16, "kd_high", 25)
         kd_low = placed(PACK * WEAVE_SLOTS, BF16, "kd_low", 22)
         nc.vector.tensor_copy(*interleaved(kd_high[:], planes[:, :, WEAVE_SLOTS:]))
         nc.scalar.copy(*interleaved(kd_low[:], planes[:, :, :WEAVE_SLOTS]))
         turn_keys(last, bank("e", 1, "k_turn3"))
-        first = slice(0, P)
-        a_rest = placed(N - P, F32, "a_rest", 16.5)
-        in_list_order(a_rest, a_all_ps, slice(P, N))
         kd_codes = tile(N, U32, "kd_codes")
         kd_scales = tile(N, U8, "kd_scales")
         for part, slots in ((kd_low, slice(0, WEAVE_SLOTS)), (kd_high, slice(WEAVE_SLOTS, N))):
@@ -225,15 +231,12 @@ def tile_attend_gttt_W_kernel(tc, kT, vT, W, ts, tk, cf, offs, out):
         b_all = placed(N, F32, "b_all", 4.5)
         in_list_order(b_all, b_all_ps, every)
         quantize_turned_keys(last, tile(P, U8, "ki_scales3"))
-        a_first = {j: tile(P, F32, "a_first%d" % j, tag="k_turned%d" % j) for j in (2, 3)}
-        for j in (2, 3):
-            in_list_order(a_first[j], a_all_ps, first)
         for j in range(1, TILES):
             first_product(j)
 
         fitted = [tile(N, F32, "fitted%d" % j, tag="v_win0" if j == 1 else None) for j in range(TILES)]
         e_rows = {j: tile(N, BF16, "e_rows%d" % j) for j in range(2, TILES)}
-        e_in = [tile(N, BF16, "e_in%d" % j, tag=tag) for j, tag in enumerate((None, "k_turned2", "v_win3", None))]
+        e_in = [tile(N, BF16, "e_in%d" % j, tag=tag) for j, tag in enumerate((None, "a_first2", "v_win3", None))]
 
         def fit(j):
             nc.vector.scalar_tensor_tensor(fitted[j][:], u_ps[j][:], cf_sq[:, j : j + 1], b_all[:], MULT, MULT)
@@ -329,7 +332,7 @@ def tile_attend_gttt_W_kernel(tc, kT, vT, W, ts, tk, cf, offs, out):
         shared_tile(2, lambda: weigh(1))
         turn_pairs(e_rows[2][:], turned[2])
         j = TILES - 1
-        e1, va = shared_tile(j, lambda: quantize_e(1, tile(P, U8, "e_scales1", tag="k_turned3")))
+        e1, va = shared_tile(j, lambda: quantize_e(1, tile(P, U8, "e_scales1", tag="a_first3")))
         weave_pairs(e_in[2][:], turned[2])
         finish(1, e1, whole, bank("a", 1, "o_ps1"), nc.scalar.copy, "o_sb1", None)
         turn_pairs(e_rows[j][:], turned[j])

@@ -228,13 +228,12 @@ def tile_attend_gttt_W_kernel(tc, kT, vT, W, ts, tk, cf, offs, out):
         first_product(0)
         lay_out(1, nc.vector.tensor_copy)
         load_values(3)
-        b_all = placed(N, F32, "b_all", 4.5)
+        b_all = placed(N, F32, "b_all", 16.5)
         in_list_order(b_all, b_all_ps, every)
-        quantize_turned_keys(last, tile(P, U8, "ki_scales3"))
         for j in range(1, TILES):
             first_product(j)
 
-        fitted = [tile(N, F32, "fitted%d" % j, tag="v_win0" if j == 1 else None) for j in range(TILES)]
+        fitted = {j: tile(N, F32, "fitted%d" % j) for j in (0, 2)}
         e_rows = {j: tile(N, BF16, "e_rows%d" % j) for j in range(2, TILES)}
         e_in = [tile(N, BF16, "e_in%d" % j, tag=tag) for j, tag in enumerate((None, "a_first2", "v_win3", None))]
 
@@ -263,12 +262,14 @@ def tile_attend_gttt_W_kernel(tc, kT, vT, W, ts, tk, cf, offs, out):
                 cols = slice(r * P, (r + 1) * P)
                 nc.tensor.matmul(sums[j][:, cols], fitted[j][:, cols], ident[:], start=r == 0, stop=False, is_transpose=True)
 
-        def added_tile(j):
-            raw = placed(N, F32, "raw%d" % j, 8.5 + 4 * j)
-            nc.scalar.activation(raw[:], listed(v_win[j], every), COPY, scale=cf_neg[:, j : j + 1])
-            for r in range(PACK):
-                cols = slice(r * P, (r + 1) * P)
-                nc.tensor.matmul(sums[j][:, cols], raw[:, r:N:PACK], ident[:], start=False, stop=r == PACK - 1, is_transpose=True)
+        def gather_scaled(j, scaled, slots):
+            nc.scalar.activation(scaled[:, slots], listed(v_win[j], slots), COPY, scale=cf_neg[:, j : j + 1])
+
+        def close_sum(j, parts):
+            for r, part in enumerate(parts):
+                nc.tensor.matmul(
+                    sums[j][:, r * P : (r + 1) * P], part, ident[:], start=False, stop=r == PACK - 1, is_transpose=True
+                )
 
         def weigh(j):
             nc.vector.tensor_tensor(
@@ -322,12 +323,28 @@ def tile_attend_gttt_W_kernel(tc, kT, vT, W, ts, tk, cf, offs, out):
             return made, va
 
         fit_dealt(0)
-        added_tile(0)
+        scaled = placed(N, F32, "scaled0", 8.5)
+        halves = (slice(0, HALF), slice(HALF, N))
+        for slots in halves:
+            gather_scaled(0, scaled, slots)
+        dealt = tile(N, F32, "dealt0")
+        for slots in halves:
+            runs = slice(slots.start // 16, slots.stop // 16)
+            nc.scalar.copy(
+                dealt[:].rearrange("p (r c i) -> p c r i", r=PACK, i=4)[:, runs],
+                scaled[:].rearrange("p (c i r) -> p c r i", r=PACK, i=4)[:, runs],
+            )
+        close_sum(0, [dealt[:, r * P : (r + 1) * P] for r in range(PACK)])
         fit(2)
-        fit(3)
+        fitted[1] = placed(N, F32, "fitted1", 6)
+        fitted[3] = placed(N, F32, "fitted3", 10)
         fit_dealt(1)
-        added_tile(1)
+        fit(3)
+        scaled = tile(N, F32, "scaled1")
+        gather_scaled(1, scaled, every)
+        close_sum(1, [scaled[:, r:N:PACK] for r in range(PACK)])
         weigh(0)
+        quantize_turned_keys(last, placed(P, U8, "ki_scales3", 20))
         finish(0, quantize_e(0, tile(P, U8, "e_scales0", tag="v_win1")), whole, bank("a", 0, "o_ps0"), nc.scalar.copy, "o_sb0", "v_win2")
         shared_tile(2, lambda: weigh(1))
         turn_pairs(e_rows[2][:], turned[2])

@@ -262,8 +262,19 @@ def tile_attend_gttt_W_kernel(tc, kT, vT, W, ts, tk, cf, offs, out):
                 cols = slice(r * P, (r + 1) * P)
                 nc.tensor.matmul(sums[j][:, cols], fitted[j][:, cols], ident[:], start=r == 0, stop=False, is_transpose=True)
 
-        def gather_scaled(j, scaled, slots):
-            nc.scalar.activation(scaled[:, slots], listed(v_win[j], slots), COPY, scale=cf_neg[:, j : j + 1])
+        def gather_and_deal(j, raw, dealt):
+            halves = (slice(0, HALF), slice(HALF, N))
+            for slots in halves:
+                nc.scalar.activation(raw[:, slots], listed(v_win[j], slots), COPY)
+            for slots in halves:
+                runs = slice(slots.start // 16, slots.stop // 16)
+                nc.scalar.activation(
+                    dealt[:].rearrange("p (r c i) -> p c r i", r=PACK, i=4)[:, runs],
+                    raw[:].rearrange("p (c i r) -> p c r i", r=PACK, i=4)[:, runs],
+                    COPY,
+                    scale=cf_neg[:, j : j + 1],
+                )
+            close_sum(j, [dealt[:, r * P : (r + 1) * P] for r in range(PACK)])
 
         def close_sum(j, parts):
             for r, part in enumerate(parts):
@@ -323,26 +334,13 @@ def tile_attend_gttt_W_kernel(tc, kT, vT, W, ts, tk, cf, offs, out):
             return made, va
 
         fit_dealt(0)
-        scaled = placed(N, F32, "scaled0", 8.5)
-        halves = (slice(0, HALF), slice(HALF, N))
-        for slots in halves:
-            gather_scaled(0, scaled, slots)
-        dealt = tile(N, F32, "dealt0")
-        for slots in halves:
-            runs = slice(slots.start // 16, slots.stop // 16)
-            nc.scalar.copy(
-                dealt[:].rearrange("p (r c i) -> p c r i", r=PACK, i=4)[:, runs],
-                scaled[:].rearrange("p (c i r) -> p c r i", r=PACK, i=4)[:, runs],
-            )
-        close_sum(0, [dealt[:, r * P : (r + 1) * P] for r in range(PACK)])
+        gather_and_deal(0, placed(N, F32, "raw0", 8.5), tile(N, F32, "dealt0"))
         fit(2)
         fitted[1] = placed(N, F32, "fitted1", 6)
         fitted[3] = placed(N, F32, "fitted3", 10)
         fit_dealt(1)
         fit(3)
-        scaled = tile(N, F32, "scaled1")
-        gather_scaled(1, scaled, every)
-        close_sum(1, [scaled[:, r:N:PACK] for r in range(PACK)])
+        gather_and_deal(1, tile(N, F32, "raw1"), tile(N, F32, "dealt1"))
         weigh(0)
         quantize_turned_keys(last, placed(P, U8, "ki_scales3", 20))
         finish(0, quantize_e(0, tile(P, U8, "e_scales0", tag="v_win1")), whole, bank("a", 0, "o_ps0"), nc.scalar.copy, "o_sb0", "v_win2")

@@ -262,15 +262,15 @@ def tile_attend_gttt_W_kernel(tc, kT, vT, W, ts, tk, cf, offs, out):
                 cols = slice(r * P, (r + 1) * P)
                 nc.tensor.matmul(sums[j][:, cols], fitted[j][:, cols], ident[:], start=r == 0, stop=False, is_transpose=True)
 
-        def gather_and_deal(j, raw, dealt):
+        def gather_and_deal(j, raws, dealt):
             halves = (slice(0, HALF), slice(HALF, N))
-            for slots in halves:
-                nc.scalar.activation(raw[:, slots], listed(v_win[j], slots), COPY)
-            for slots in halves:
+            for raw, slots in zip(raws, halves):
+                nc.scalar.activation(raw[:], listed(v_win[j], slots), COPY)
+            for raw, slots in zip(raws, halves):
                 runs = slice(slots.start // 16, slots.stop // 16)
                 nc.scalar.activation(
                     dealt[:].rearrange("p (r c i) -> p c r i", r=PACK, i=4)[:, runs],
-                    raw[:].rearrange("p (c i r) -> p c r i", r=PACK, i=4)[:, runs],
+                    raw[:].rearrange("p (c i r) -> p c r i", r=PACK, i=4),
                     COPY,
                     scale=cf_neg[:, j : j + 1],
                 )
@@ -334,16 +334,16 @@ def tile_attend_gttt_W_kernel(tc, kT, vT, W, ts, tk, cf, offs, out):
             return made, va
 
         fit_dealt(0)
-        gather_and_deal(0, placed(N, F32, "raw0", 8.5), tile(N, F32, "dealt0"))
+        gather_and_deal(0, [placed(HALF, F32, "raw0a", 8.5), placed(HALF, F32, "raw0b", 10.5)], tile(N, F32, "dealt0"))
         fit(2)
         fitted[1] = placed(N, F32, "fitted1", 6)
         fitted[3] = placed(N, F32, "fitted3", 10)
         fit_dealt(1)
         fit(3)
-        gather_and_deal(1, tile(N, F32, "raw1"), tile(N, F32, "dealt1"))
+        gather_and_deal(1, [tile(HALF, F32, "raw1a"), tile(HALF, F32, "raw1b")], tile(N, F32, "dealt1"))
         weigh(0)
         quantize_turned_keys(last, placed(P, U8, "ki_scales3", 20))
-        finish(0, quantize_e(0, tile(P, U8, "e_scales0", tag="v_win1")), whole, bank("a", 0, "o_ps0"), nc.scalar.copy, "o_sb0", "v_win2")
+        finish(0, quantize_e(0, tile(P, U8, "e_scales0", tag="raw1a")), whole, bank("a", 0, "o_ps0"), nc.scalar.copy, "o_sb0", "v_win2")
         shared_tile(2, lambda: weigh(1))
         turn_pairs(e_rows[2][:], turned[2])
         j = TILES - 1

@@ -11,7 +11,9 @@ TILES = N // P
 HALF = N // 2
 WEAVE_SLOTS = 128
 KEY_SLOTS = 192
-VALUE_SLOTS = {2: 256, 3: 288}
+VECTOR_CUTS = {2: (0, 192), 3: (0, 160, 288)}
+SCALAR_CUTS = {2: (192, 384, 512), 3: (288, 416, 512)}
+WINDOW_AT = {2: 80, 3: 96}
 LAST = P - 1
 TS_ROW = P // 2 - 1
 
@@ -122,12 +124,6 @@ def tile_attend_gttt_W_kernel(tc, kT, vT, W, ts, tk, cf, offs, out):
                 nc.tensor.transpose(spread_ps[:, c * P : (c + 1) * P], col[:, c : c + 1].to_broadcast([P, P]), ident[:])
             return spread_ps
 
-        def in_list_order(rows, dealt_ps, slots):
-            nc.scalar.copy(
-                rows[:].rearrange("p (s r) -> p s r", r=PACK),
-                dealt_ps[:].rearrange("p (r s) -> p s r", r=PACK)[:, slots.start // PACK : slots.stop // PACK],
-            )
-
         tk_row = tile(N, F32, "tk_row")
         nc.scalar.activation(tk_row[:], listed(tk_win, every), COPY)
         ts_row = tile(N, F32, "ts_row")
@@ -148,14 +144,12 @@ def tile_attend_gttt_W_kernel(tc, kT, vT, W, ts, tk, cf, offs, out):
         for c in range(TILES):
             at = c * P + TS_ROW
             nc.scalar.activation(a_col[:, c : c + 1], ts_ps[:, at : at + 1], COPY, scale=tk_col[:, c : c + 1])
-        b_col = tile(TILES, F32, "b_col")
-        for c in range(TILES):
-            nc.scalar.activation(b_col[:, c : c + 1], tk_col[:, c : c + 1], COPY, scale=a_col[:, c : c + 1])
 
         v_win = []
 
         def load_values(j):
-            v_win.append(tile(T, F32, "v_win%d" % j))
+            name = "v_win%d" % j
+            v_win.append(placed(T, F32, name, WINDOW_AT[j]) if j in WINDOW_AT else tile(T, F32, name))
             nc.sync.dma_start(v_win[j][:], vT[j * P : (j + 1) * P, :])
 
         load_values(0)
@@ -170,15 +164,6 @@ def tile_attend_gttt_W_kernel(tc, kT, vT, W, ts, tk, cf, offs, out):
         nc.scalar.activation(cf_neg[:], cf_ps[:, P - TILES : P], COPY, scale=-1.0)
         cf_sq = tile(TILES, F32, "cf_sq")
         nc.scalar.activation(cf_sq[:], cf_ps[:, P - TILES : P], SQUARE)
-
-        a_all_ps = spread(a_col, "a_all", "e", 2)
-        b_all_ps = spread(b_col, "b_all", "e", 3)
-        first = slice(0, P)
-        a_first = {j: tile(P, F32, "a_first%d" % j) for j in (2, 3)}
-        for j in (2, 3):
-            in_list_order(a_first[j], a_all_ps, first)
-        a_rest = tile(N - P, F32, "a_rest")
-        in_list_order(a_rest, a_all_ps, slice(P, N))
 
         gather_keys(2)
         load_values(2)
@@ -205,7 +190,7 @@ def tile_attend_gttt_W_kernel(tc, kT, vT, W, ts, tk, cf, offs, out):
             nc.vector.quantize_mx(kd_codes[:, slots].bitcast(E4M3), kd_scales[:, slots], part[:])
 
         w_planes = w_raw[:].rearrange("p (t f) -> p t f", t=PACK)
-        w_in = [placed(N, BF16, "w_in%d" % j, (20.5, 23, 8.5, 12.5)[j]) for j in range(TILES)]
+        w_in = [placed(N, BF16, "w_in%d" % j, (8.5, 7.5, 9.75, 12.5)[j]) for j in range(TILES)]
         u_ps = []
 
         def lay_out(j, copy):
@@ -221,66 +206,61 @@ def tile_attend_gttt_W_kernel(tc, kT, vT, W, ts, tk, cf, offs, out):
                 rhs=kd_codes[:].bitcast(E4M3), rhs_scale=kd_scales[:], start=True, stop=True,
             )
 
-        lay_out(0, nc.vector.tensor_copy)
-        lay_out(2, nc.scalar.copy)
+        lay_out(0, nc.scalar.copy)
         lay_out(3, nc.scalar.copy)
         quantize_turned_keys(2, placed(P, U8, "ki_scales2", 22.5))
         first_product(0)
         lay_out(1, nc.vector.tensor_copy)
+        lay_out(2, nc.vector.tensor_copy)
         load_values(3)
-        b_all = placed(N, F32, "b_all", 16.5)
-        in_list_order(b_all, b_all_ps, every)
         for j in range(1, TILES):
             first_product(j)
 
-        fitted = {j: tile(N, F32, "fitted%d" % j) for j in (0, 2)}
-        e_rows = {j: tile(N, BF16, "e_rows%d" % j) for j in range(2, TILES)}
-        e_in = [tile(N, BF16, "e_in%d" % j, tag=tag) for j, tag in enumerate((None, "a_first2", "v_win3", None))]
+        quantize_turned_keys(last, placed(P, U8, "ki_scales3", 12.5))
+        sums = [bank(*at, "e_sum%d" % j) for j, at in enumerate((("e", 0), ("a", 2), ("e", 2), ("e", 3)))]
+        dealt = [tile(N, F32, "dealt%d" % j) for j in range(TILES)]
+        e_in = [tile(N, BF16, "e_in0"), placed(N, BF16, "e_in1", WINDOW_AT[2]), placed(N, BF16, "e_in2", WINDOW_AT[3]), tile(N, BF16, "e_in3")]
+
+        def add_turned(j, rows, first):
+            for r in range(PACK):
+                cols = slice(r * P, (r + 1) * P)
+                nc.tensor.matmul(
+                    sums[j][:, cols], rows[:, cols], ident[:],
+                    start=first and r == 0, stop=not first and r == PACK - 1, is_transpose=True,
+                )
 
         def fit(j):
-            nc.vector.scalar_tensor_tensor(fitted[j][:], u_ps[j][:], cf_sq[:, j : j + 1], b_all[:], MULT, MULT)
-
-        def residual(j, va, slots):
+            name = "fitted%d" % j
+            fitted = placed(N, F32, name, {2: 130.5, 3: 135}[j]) if j >= 2 else tile(N, F32, name)
             nc.vector.scalar_tensor_tensor(
-                e_rows[j][:, slots], va, cf_neg[:, j : j + 1], fitted[j][:, slots], MULT, ADD
-            )
-
-        turned = {j: bank("e", j, "e_turn%d" % j) for j in range(2, TILES)}
-        sums = {}
-
-        def fit_dealt(j):
-            nc.vector.scalar_tensor_tensor(
-                fitted[j][:].rearrange("p (r s) -> p r s", r=PACK),
+                fitted[:].rearrange("p (r s) -> p r s", r=PACK),
                 u_ps[j][:].rearrange("p (s r) -> p r s", r=PACK),
                 cf_sq[:, j : j + 1],
                 tk_dealt[:].rearrange("p (r s) -> p r s", r=PACK),
                 MULT,
                 MULT,
             )
-            sums[j] = bank("e", j, "e_sum%d" % j)
-            for r in range(PACK):
-                cols = slice(r * P, (r + 1) * P)
-                nc.tensor.matmul(sums[j][:, cols], fitted[j][:, cols], ident[:], start=r == 0, stop=False, is_transpose=True)
+            add_turned(j, fitted, True)
 
-        def gather_and_deal(j, raws, dealt):
-            halves = (slice(0, HALF), slice(HALF, N))
-            for raw, slots in zip(raws, halves):
-                nc.scalar.activation(raw[:], listed(v_win[j], slots), COPY)
-            for raw, slots in zip(raws, halves):
-                runs = slice(slots.start // 16, slots.stop // 16)
-                nc.scalar.activation(
-                    dealt[:].rearrange("p (r c i) -> p c r i", r=PACK, i=4)[:, runs],
-                    raw[:].rearrange("p (c i r) -> p c r i", r=PACK, i=4),
-                    COPY,
-                    scale=cf_neg[:, j : j + 1],
-                )
-            close_sum(j, [dealt[:, r * P : (r + 1) * P] for r in range(PACK)])
+        def scalar_gather(raw, window):
+            nc.scalar.activation(raw, window, COPY)
 
-        def close_sum(j, parts):
-            for r, part in enumerate(parts):
-                nc.tensor.matmul(
-                    sums[j][:, r * P : (r + 1) * P], part, ident[:], start=False, stop=r == PACK - 1, is_transpose=True
-                )
+        def scalar_deal(dst, src, factor):
+            nc.scalar.activation(dst, src, COPY, scale=factor)
+
+        def gather_values(j, shares):
+            raws = []
+            for n, (slots, gather, at) in enumerate(shares):
+                raws.append(placed(slots.stop - slots.start, F32, "raw%d_%d" % (j, n), at))
+                gather(raws[n][:], listed(v_win[j], slots))
+            return raws
+
+        def deal(j, raw, slots, scale):
+            scale(
+                dealt[j][:].rearrange("p (r c i) -> p c r i", r=PACK, i=4)[:, slots.start // 16 : slots.stop // 16],
+                raw[:].rearrange("p (c i r) -> p c r i", r=PACK, i=4),
+                cf_neg[:, j : j + 1],
+            )
 
         def weigh(j):
             nc.vector.tensor_tensor(
@@ -311,53 +291,68 @@ def tile_attend_gttt_W_kernel(tc, kT, vT, W, ts, tk, cf, offs, out):
                 o_sb[:].rearrange("p (t f) -> p t f", t=len(planes)),
             )
 
-        def finish(j, quantised, planes, o_ps, copy, name, tag):
-            products(quantised, planes, o_ps)
-            width = P * len(planes)
-            o_sb = tile(width, F32, name, tag=tag)
-            copy(o_sb[:], o_ps[:, :width])
-            store(j, planes, o_sb)
-
         whole = range(PACK)
-        def shared_tile(j, between):
-            cut = VALUE_SLOTS[j]
-            second, mine, theirs = slice(P, cut), slice(0, cut), slice(cut, N)
-            raw = tile(N - cut, F32, "raw%d" % j)
-            va = tile(N, F32, "va%d" % j)
-            nc.scalar.activation(raw[:], listed(v_win[j], theirs), COPY)
-            nc.vector.tensor_tensor(va[:, first], listed(v_win[j], first), a_first[j][:], MULT)
-            nc.vector.tensor_tensor(va[:, second], listed(v_win[j], second), a_rest[:, : cut - P], MULT)
-            made = between()
-            nc.vector.tensor_tensor(va[:, theirs], raw[:], a_rest[:, cut - P :], MULT)
-            residual(j, va[:, mine], mine)
-            residual(j, va[:, theirs], theirs)
-            return made, va
+        halves = (slice(0, HALF), slice(HALF, N))
 
-        fit_dealt(0)
-        gather_and_deal(0, [placed(HALF, F32, "raw0a", 8.5), placed(HALF, F32, "raw0b", 10.5)], tile(N, F32, "dealt0"))
-        fit(2)
-        fitted[1] = placed(N, F32, "fitted1", 6)
-        fitted[3] = placed(N, F32, "fitted3", 10)
-        fit_dealt(1)
-        fit(3)
-        gather_and_deal(1, [tile(HALF, F32, "raw1a"), tile(HALF, F32, "raw1b")], tile(N, F32, "dealt1"))
+        def scalar_tile(j, at):
+            raws = gather_values(j, [(slots, scalar_gather, at + 6 * n) for n, slots in enumerate(halves)])
+            for raw, slots in zip(raws, halves):
+                deal(j, raw, slots, scalar_deal)
+            add_turned(j, dealt[j], False)
+
+
+        def shared_tile(j, at):
+            parts = [
+                (slice(a, b), gather, scale)
+                for cuts, gather, scale in (
+                    (VECTOR_CUTS[j], nc.vector.tensor_copy, nc.vector.tensor_scalar_mul),
+                    (SCALAR_CUTS[j], scalar_gather, scalar_deal),
+                )
+                for a, b in zip(cuts, cuts[1:])
+            ]
+            raws = gather_values(j, [(slots, gather, at + 2 * n) for n, (slots, gather, scale) in enumerate(parts)])
+            for raw, (slots, gather, scale) in zip(raws, parts):
+                deal(j, raw, slots, scale)
+            add_turned(j, dealt[j], False)
+
+        def early_output(j, quantised, at):
+            o_ps = bank("a", j, "o_ps%d" % j)
+            products(quantised, whole, o_ps)
+            o_sb = placed(N, F32, "o_sb%d" % j, at)
+            nc.scalar.copy(o_sb[:], o_ps[:])
+            store(j, whole, o_sb)
+
+        fit(0)
+        scalar_tile(0, 134)
+        for j in range(1, TILES):
+            fit(j)
+        scalar_tile(1, 40)
         weigh(0)
-        quantize_turned_keys(last, placed(P, U8, "ki_scales3", 20))
-        finish(0, quantize_e(0, tile(P, U8, "e_scales0", tag="raw1a")), whole, bank("a", 0, "o_ps0"), nc.scalar.copy, "o_sb0", "v_win2")
-        shared_tile(2, lambda: weigh(1))
-        turn_pairs(e_rows[2][:], turned[2])
+        e0 = quantize_e(0, placed(P, U8, "e_scales0", 40))
+
+        shared_tile(2, 114)
+        weigh(1)
+        early_output(0, e0, WINDOW_AT[2] + 4)
+        e1 = quantize_e(1, tile(P, U8, "e_scales1"))
+
         j = TILES - 1
-        e1, va = shared_tile(j, lambda: quantize_e(1, tile(P, U8, "e_scales1", tag="a_first3")))
-        weave_pairs(e_in[2][:], turned[2])
-        finish(1, e1, whole, bank("a", 1, "o_ps1"), nc.scalar.copy, "o_sb1", None)
-        turn_pairs(e_rows[j][:], turned[j])
-        e2 = quantize_e(2, tile(P, U8, "e_scales2", tag="va3"))
-        weave_pairs(e_in[j][:], turned[j])
+        shared_tile(j, 122)
+        early_output(1, e1, WINDOW_AT[j] + 4)
+        weigh(2)
+        e2 = quantize_e(2, tile(P, U8, "e_scales2"))
+        weigh(j)
         e3 = quantize_e(j, tile(P, U8, "e_scales3"))
         o_sb = tile(N, F32, "o_sb2")
         for h, o_ps in enumerate((bank("a", 2, "o_ps2"), bank("e", 1, "o_ps2b"))):
             products(e2, (2 * h, 2 * h + 1), o_ps)
             nc.scalar.copy(o_sb[:, h * HALF : (h + 1) * HALF], o_ps[:, :HALF])
         store(2, whole, o_sb)
-        finish(j, e3, (0, 1), bank("a", 3, "o_ps3"), nc.vector.tensor_copy, "o_sb3", None)
-        finish(j, e3, (2, 3), bank("e", 0, "o_ps4"), nc.scalar.copy, "o_sb4", None)
+        last_banks = (("a", 3), ("e", 0), ("a", 0), ("a", 1))
+        for h in range(2):
+            o_sb = tile(HALF, F32, "o_sb3_%d" % h)
+            for n, copy in enumerate((nc.scalar.copy, nc.vector.tensor_copy)):
+                t = 2 * h + n
+                o_ps = bank(*last_banks[t], "o_ps3_%d" % t)
+                products(e3, (t,), o_ps)
+                copy(o_sb[:, n * P : (n + 1) * P], o_ps[:, :P])
+            store(j, (2 * h, 2 * h + 1), o_sb)

from contextlib import ExitStack

import concourse.mybir as mybir
from concourse.masks import make_identity

P = 128
PACK = 4
N = 512
T = 2048
TILES = N // P
HALF = N // 2
WEAVE_SLOTS = 128
KEY_SLOTS = 192
VECTOR_CUTS = {2: (0, 192), 3: (0, 160, 288)}
SCALAR_CUTS = {2: (192, 384, 512), 3: (288, 416, 512)}
WINDOW_AT = {2: 80, 3: 96}
LAST = P - 1
TS_ROW = P // 2 - 1

FLOPS = 2 * 2 * N * N * N
BYTES = 4 * (2 * N * T + 2 * N * N + 2 * T + N) + 2 * P * (N // 16)

F32 = mybir.dt.float32
BF16 = mybir.dt.bfloat16
U32 = mybir.dt.uint32
U16 = mybir.dt.uint16
U8 = mybir.dt.uint8
E4M3 = mybir.dt.float8_e4m3fn_x4
E5M2 = mybir.dt.float8_e5m2_x4
MULT = mybir.AluOpType.mult
ADD = mybir.AluOpType.add
COPY = mybir.ActivationFunctionType.Copy
SQUARE = mybir.ActivationFunctionType.Square


def interleaved(grouped, planes):
    dst = grouped.rearrange("p (c i t) -> p c t i", i=4, t=PACK)
    src = planes.rearrange("p t (c i) -> p c t i", i=4)
    return dst, src


def tile_attend_gttt_W_kernel(tc, kT, vT, W, ts, tk, cf, offs, out):
    nc = tc.nc
    with ExitStack() as ctx:
        sb = ctx.enter_context(tc.tile_pool(name="sb", bufs=1))
        reuse = ctx.enter_context(tc.tile_pool(name="reuse", bufs=1))
        ps = ctx.enter_context(tc.psum_pool(name="ps", bufs=1))

        def placed(cols, dtype, name, at):
            return reuse.tile([P, cols], dtype, name=name, align_bytes=64, offset=int(512 * at))

        def bank(group, j, name):
            return ps.tile([P, N], F32, name=name, tag="bank_%s%d" % (group, j))

        def tile(cols, dtype, name, tag=None):
            return sb.tile([P, cols], dtype, name=name, tag=tag or name, align_bytes=64)

        offsets = sb.tile([P, N // 16], U16, name="offsets")

        def listed(window, slots):
            return window[:].indirect(offsets[:, slots.start // 16 : slots.stop // 16])

        nc.sync.dma_start(offsets[:], offs)
        every = slice(0, N)
        tk_win = tile(T, F32, "tk_win")
        ts_win = placed(T, F32, "ts_win", 60)
        cf_rows = tile(P, F32, "cf_rows")
        ident = tile(P, F32, "ident")

        nc.gpsimd.memset(cf_rows[: P - TILES, :], 0.0)
        nc.vector.memset(tk_win[:LAST, :].bitcast(U32), 0)
        nc.vector.memset(ts_win[:TS_ROW, :].bitcast(U32), 0)
        make_identity(nc, ident[:])
        nc.gpsimd.memset(ts_win[TS_ROW + 1 :, :], 0.0)
        nc.scalar.dma_start(tk_win[LAST:, :], tk[0:1, :])
        nc.scalar.dma_start(ts_win[TS_ROW : TS_ROW + 1, :], ts[0:1, :])

        k_rows = kT.rearrange("(p t) n -> t p n", t=PACK)
        k_win = []

        def load_keys(t):
            k_win.append(tile(T, F32, "k_win%d" % t))
            nc.sync.dma_start(k_win[t][:], k_rows[t])

        load_keys(0)
        nc.sync.dma_start(cf_rows[P - TILES :, :], cf.rearrange("(j p) o -> j (p o)", p=P))
        for t in range(1, PACK):
            load_keys(t)

        def turn_pairs(src, turned):
            words = src.bitcast(F32)
            for u in range(2):
                nc.tensor.transpose(turned[:, u * P : (u + 1) * P], words[:, u : 2 * P : 2], ident[:])

        def turn_row(row, turned):
            for c in range(TILES):
                nc.tensor.transpose(turned[:, c * P : (c + 1) * P], row[:, c:N:PACK], ident[:])

        def weave_pairs(dst, turned):
            nc.scalar.copy(
                dst.bitcast(F32).rearrange("s (m u) -> s m u", u=2),
                turned[:, : 2 * P].rearrange("s (u m) -> s m u", u=2),
            )

        k_planes = placed(PACK * N + KEY_SLOTS, BF16, "k_planes", 8)
        k_turned = [placed(N, BF16, "k_turned0", 60)[:], k_planes[:, 3 * N + KEY_SLOTS :], None, tile(N, BF16, "k_turned3")[:]]
        ki_codes = [tile(P, U32, "ki_codes%d" % t) for t in range(PACK)]
        ki_scales = []

        def quantize_turned_keys(t, scales):
            ki_scales.append(scales)
            nc.vector.quantize_mx(ki_codes[t][:].bitcast(E4M3), scales[:], k_turned[t])

        def turn_keys(t, turned):
            turn_pairs(k_planes[:, t * N : (t + 1) * N], turned)
            weave_pairs(k_turned[t], turned)

        def gather_keys(t):
            nc.vector.tensor_copy(k_planes[:, t * N : (t + 1) * N], listed(k_win[t], every))

        def spread(col, name, group, j):
            spread_ps = bank(group, j, name + "_ps")
            for c in range(TILES):
                nc.tensor.transpose(spread_ps[:, c * P : (c + 1) * P], col[:, c : c + 1].to_broadcast([P, P]), ident[:])
            return spread_ps

        tk_row = tile(N, F32, "tk_row")
        nc.scalar.activation(tk_row[:], listed(tk_win, every), COPY)
        ts_row = tile(N, F32, "ts_row")
        nc.scalar.activation(ts_row[:], listed(ts_win, every), COPY)
        tk_ps = bank("a", 0, "tk_ps")
        turn_row(tk_row, tk_ps)
        tk_col = placed(TILES, F32, "tk_col", 62)
        nc.scalar.copy(tk_col[:], tk_ps[:, LAST:N:P])
        ts_ps = bank("a", 1, "ts_ps")
        turn_row(ts_row, ts_ps)
        gather_keys(0)
        w_raw = tile(PACK * N, F32, "w_raw")
        nc.sync.dma_start(w_raw[:], W.rearrange("(p t) f -> p (t f)", t=PACK))
        turn_keys(0, bank("e", 0, "k_turn0"))
        tk_dealt = tile(N, F32, "tk_dealt")
        nc.scalar.copy(tk_dealt[:], spread(tk_col, "tk_dealt", "a", 2)[:])
        a_col = tile(TILES, F32, "a_col")
        for c in range(TILES):
            at = c * P + TS_ROW
            nc.scalar.activation(a_col[:, c : c + 1], ts_ps[:, at : at + 1], COPY, scale=tk_col[:, c : c + 1])

        v_win = []

        def load_values(j):
            name = "v_win%d" % j
            v_win.append(placed(T, F32, name, WINDOW_AT[j]) if j in WINDOW_AT else tile(T, F32, name))
            nc.sync.dma_start(v_win[j][:], vT[j * P : (j + 1) * P, :])

        load_values(0)
        gather_keys(1)
        load_values(1)
        quantize_turned_keys(0, tile(P, U8, "ki_scales0", tag="k_win1"))
        turn_keys(1, bank("e", 1, "k_turn1"))

        cf_ps = bank("a", 0, "cf_ps")
        nc.tensor.transpose(cf_ps[:, :P], cf_rows[:], ident[:])
        cf_neg = tile(TILES, F32, "cf_neg")
        nc.scalar.activation(cf_neg[:], cf_ps[:, P - TILES : P], COPY, scale=-1.0)
        cf_sq = tile(TILES, F32, "cf_sq")
        nc.scalar.activation(cf_sq[:], cf_ps[:, P - TILES : P], SQUARE)

        gather_keys(2)
        load_values(2)
        quantize_turned_keys(1, tile(P, U8, "ki_scales1", tag="k_win2"))
        turned2 = bank("e", 2, "k_turn2")
        turn_pairs(k_planes[:, 2 * N : 3 * N], turned2)

        last = PACK - 1
        plane = k_planes[:, last * N : PACK * N]
        nc.vector.tensor_copy(plane[:, KEY_SLOTS:], listed(k_win[last], slice(KEY_SLOTS, N)))
        nc.scalar.activation(plane[:, :KEY_SLOTS], listed(k_win[last], slice(0, KEY_SLOTS)), COPY)

        k_turned[2] = tile(N, BF16, "k_turned2", tag="k_win3")[:]
        weave_pairs(k_turned[2], turned2)
        planes = k_planes[:, : PACK * N].rearrange("p (t n) -> p t n", t=PACK)
        kd_high = placed(PACK * (N - WEAVE_SLOTS), BF16, "kd_high", 25)
        kd_low = placed(PACK * WEAVE_SLOTS, BF16, "kd_low", 22)
        nc.vector.tensor_copy(*interleaved(kd_high[:], planes[:, :, WEAVE_SLOTS:]))
        nc.scalar.copy(*interleaved(kd_low[:], planes[:, :, :WEAVE_SLOTS]))
        turn_keys(last, bank("e", 1, "k_turn3"))
        kd_codes = tile(N, U32, "kd_codes")
        kd_scales = tile(N, U8, "kd_scales")
        for part, slots in ((kd_low, slice(0, WEAVE_SLOTS)), (kd_high, slice(WEAVE_SLOTS, N))):
            nc.vector.quantize_mx(kd_codes[:, slots].bitcast(E4M3), kd_scales[:, slots], part[:])

        w_planes = w_raw[:].rearrange("p (t f) -> p t f", t=PACK)
        w_in = [placed(N, BF16, "w_in%d" % j, (8.5, 7.5, 9.75, 12.5)[j]) for j in range(TILES)]
        u_ps = []

        def lay_out(j, copy):
            copy(*interleaved(w_in[j][:], w_planes[:, :, j * P : (j + 1) * P]))

        def first_product(j):
            w_codes = tile(P, U32, "w_codes%d" % j)
            w_scales = tile(P, U8, "w_scales%d" % j)
            nc.vector.quantize_mx(w_codes[:].bitcast(E4M3), w_scales[:], w_in[j][:])
            u_ps.append(bank("a", j, "u_ps%d" % j))
            nc.tensor.matmul_mx(
                out=u_ps[j][:], lhsT=w_codes[:].bitcast(E4M3), lhsT_scale=w_scales[:],
                rhs=kd_codes[:].bitcast(E4M3), rhs_scale=kd_scales[:], start=True, stop=True,
            )

        lay_out(0, nc.scalar.copy)
        lay_out(3, nc.scalar.copy)
        quantize_turned_keys(2, placed(P, U8, "ki_scales2", 22.5))
        first_product(0)
        lay_out(1, nc.vector.tensor_copy)
        lay_out(2, nc.vector.tensor_copy)
        load_values(3)
        for j in range(1, TILES):
            first_product(j)

        quantize_turned_keys(last, placed(P, U8, "ki_scales3", 12.5))
        sums = [bank(*at, "e_sum%d" % j) for j, at in enumerate((("e", 0), ("a", 2), ("e", 2), ("e", 3)))]
        dealt = [tile(N, F32, "dealt%d" % j) for j in range(TILES)]
        e_in = [tile(N, BF16, "e_in0"), placed(N, BF16, "e_in1", WINDOW_AT[2]), placed(N, BF16, "e_in2", WINDOW_AT[3]), tile(N, BF16, "e_in3")]

        def add_turned(j, rows, first):
            for r in range(PACK):
                cols = slice(r * P, (r + 1) * P)
                nc.tensor.matmul(
                    sums[j][:, cols], rows[:, cols], ident[:],
                    start=first and r == 0, stop=not first and r == PACK - 1, is_transpose=True,
                )

        def fit(j):
            name = "fitted%d" % j
            fitted = placed(N, F32, name, {2: 130.5, 3: 135}[j]) if j >= 2 else tile(N, F32, name)
            nc.vector.scalar_tensor_tensor(
                fitted[:].rearrange("p (r s) -> p r s", r=PACK),
                u_ps[j][:].rearrange("p (s r) -> p r s", r=PACK),
                cf_sq[:, j : j + 1],
                tk_dealt[:].rearrange("p (r s) -> p r s", r=PACK),
                MULT,
                MULT,
            )
            add_turned(j, fitted, True)

        def scalar_gather(raw, window):
            nc.scalar.activation(raw, window, COPY)

        def scalar_deal(dst, src, factor):
            nc.scalar.activation(dst, src, COPY, scale=factor)

        def gather_values(j, shares):
            raws = []
            for n, (slots, gather, at) in enumerate(shares):
                raws.append(placed(slots.stop - slots.start, F32, "raw%d_%d" % (j, n), at))
                gather(raws[n][:], listed(v_win[j], slots))
            return raws

        def deal(j, raw, slots, scale):
            scale(
                dealt[j][:].rearrange("p (r c i) -> p c r i", r=PACK, i=4)[:, slots.start // 16 : slots.stop // 16],
                raw[:].rearrange("p (c i r) -> p c r i", r=PACK, i=4),
                cf_neg[:, j : j + 1],
            )

        def weigh(j):
            nc.vector.tensor_tensor(
                e_in[j][:].rearrange("s (m r) -> s m r", r=PACK),
                sums[j][:].rearrange("s (r m) -> s m r", r=PACK),
                a_col[:].unsqueeze(1).to_broadcast([P, P, PACK]),
                MULT,
            )

        def quantize_e(j, scales):
            codes = tile(P, U32, "e_codes%d" % j)
            nc.vector.quantize_mx(codes[:].bitcast(E5M2), scales[:], e_in[j][:])
            return codes, scales

        out_rows = out.rearrange("(p t) f -> p t f", t=PACK)

        def products(quantised, planes, o_ps):
            codes, scales = quantised
            for n, t in enumerate(planes):
                nc.tensor.matmul_mx(
                    out=o_ps[:, n * P : (n + 1) * P], lhsT=ki_codes[t][:].bitcast(E4M3), lhsT_scale=ki_scales[t][:],
                    rhs=codes[:].bitcast(E5M2), rhs_scale=scales[:], start=True, stop=True,
                )

        def store(j, planes, o_sb):
            nc.sync.dma_start(
                out_rows[:, planes[0] : planes[-1] + 1, j * P : (j + 1) * P],
                o_sb[:].rearrange("p (t f) -> p t f", t=len(planes)),
            )

        whole = range(PACK)
        halves = (slice(0, HALF), slice(HALF, N))

        def scalar_tile(j, at):
            raws = gather_values(j, [(slots, scalar_gather, at + 6 * n) for n, slots in enumerate(halves)])
            for raw, slots in zip(raws, halves):
                deal(j, raw, slots, scalar_deal)
            add_turned(j, dealt[j], False)


        def shared_tile(j, at):
            parts = [
                (slice(a, b), gather, scale)
                for cuts, gather, scale in (
                    (VECTOR_CUTS[j], nc.vector.tensor_copy, nc.vector.tensor_scalar_mul),
                    (SCALAR_CUTS[j], scalar_gather, scalar_deal),
                )
                for a, b in zip(cuts, cuts[1:])
            ]
            raws = gather_values(j, [(slots, gather, at + 2 * n) for n, (slots, gather, scale) in enumerate(parts)])
            for raw, (slots, gather, scale) in zip(raws, parts):
                deal(j, raw, slots, scale)
            add_turned(j, dealt[j], False)

        def early_output(j, quantised, at):
            o_ps = bank("a", j, "o_ps%d" % j)
            products(quantised, whole, o_ps)
            o_sb = placed(N, F32, "o_sb%d" % j, at)
            nc.scalar.copy(o_sb[:], o_ps[:])
            store(j, whole, o_sb)

        fit(0)
        scalar_tile(0, 134)
        for j in range(1, TILES):
            fit(j)
        scalar_tile(1, 40)
        weigh(0)
        e0 = quantize_e(0, placed(P, U8, "e_scales0", 40))

        shared_tile(2, 114)
        weigh(1)
        early_output(0, e0, WINDOW_AT[2] + 4)
        e1 = quantize_e(1, tile(P, U8, "e_scales1"))

        j = TILES - 1
        shared_tile(j, 122)
        early_output(1, e1, WINDOW_AT[j] + 4)
        weigh(2)
        e2 = quantize_e(2, tile(P, U8, "e_scales2"))
        weigh(j)
        e3 = quantize_e(j, tile(P, U8, "e_scales3"))
        o_sb = tile(N, F32, "o_sb2")
        for h, o_ps in enumerate((bank("a", 2, "o_ps2"), bank("e", 1, "o_ps2b"))):
            products(e2, (2 * h, 2 * h + 1), o_ps)
            nc.scalar.copy(o_sb[:, h * HALF : (h + 1) * HALF], o_ps[:, :HALF])
        store(2, whole, o_sb)
        last_banks = (("a", 3), ("e", 0), ("a", 0), ("a", 1))
        for h in range(2):
            o_sb = tile(HALF, F32, "o_sb3_%d" % h)
            for n, copy in enumerate((nc.scalar.copy, nc.vector.tensor_copy)):
                t = 2 * h + n
                o_ps = bank(*last_banks[t], "o_ps3_%d" % t)
                products(e3, (t,), o_ps)
                copy(o_sb[:, n * P : (n + 1) * P], o_ps[:, :P])
            store(j, (2 * h, 2 * h + 1), o_sb)
